import numpy as np
import ml_dtypes


def mxq(x, axis, fmt="e4m3"):
    dtype, down = {"e4m3": (ml_dtypes.float8_e4m3fn, 7), "e5m2": (ml_dtypes.float8_e5m2, 14)}[fmt]
    v = np.moveaxis(np.asarray(x, np.float32).astype(ml_dtypes.bfloat16).astype(np.float64), axis, -1)
    blocks = v.reshape(v.shape[:-1] + (-1, 32))
    amax = np.abs(blocks).max(-1, keepdims=True)
    byte = np.maximum(np.where(amax > 0, np.frexp(amax)[1] - 1 + 127, 0) - down, 1)
    scale = np.exp2(byte - 127.0)
    codes = (blocks / scale).astype(np.float32).astype(dtype).astype(np.float64)
    return np.moveaxis((codes * scale).reshape(v.shape), -1, axis)


WIDE = False


def mx_kscale(k):
    if not WIDE:
        return np.ones(k)
    levels = np.array([10, -10, 5, -5, 0])
    if k % 512:
        return np.exp2(np.random.permutation(np.resize(levels, k // 32))).repeat(32)
    a = np.empty((k // 512, 16))
    for p in range(k // 512):
        a[p, :8] = np.random.permutation(np.resize(levels, 8))
        for g in range(8):
            far = levels[np.abs(levels - a[p, g]) >= 10]
            a[p, g + 8] = far[np.random.randint(len(far))]
    return np.exp2(a.ravel()).repeat(32)


def f64(x):
    return np.asarray(x).astype(np.float64)


def striped(idx):
    return np.tile(idx.reshape(-1, 16).T, (8, 1)).astype(np.uint16)


def unstriped(offs):
    return offs[:16].T.reshape(-1).astype(np.int64)


def silu(v):
    return v / (1.0 + np.exp(-np.maximum(v, -700.0)))


K, T, S, N, U = 1024, 2048, 512, 256, 1024


def setup_inputs():
    n = np.random.standard_normal
    s = mx_kscale(K)[:, None]
    return {
        "xT": (n((K, T)) * s).astype(np.float32),
        "w1": (n((K, N)) / np.sqrt(K) / s).astype(np.float32),
        "gamma": np.random.uniform(0.5, 1.5, (N, U)).astype(np.float32),
        "beta": (0.5 * n((N, U))).astype(np.float32),
        "offs": striped(np.random.permutation(T)[:S]),
        "cls": striped(np.random.randint(0, U, S)),
    }


def reference(xT, w1, gamma, beta, offs, cls):
    xq = mxq(f64(xT)[:, unstriped(offs)], 0, "e4m3")
    y = mxq(f64(w1), 0, "e4m3").T @ xq
    g = f64(gamma)[:, unstriped(cls)]
    s = f64(beta)[:, unstriped(cls)]
    return silu(y * g + s)

@@ -1,0 +1,171 @@
+from contextlib import ExitStack
+
+import concourse.mybir as mybir
+
+K, T, S, N, U = 1024, 2048, 512, 256, 1024
+FLOPS = 2 * K * S * N
+
+F32 = mybir.dt.float32
+BF16 = mybir.dt.bfloat16
+U32 = mybir.dt.uint32
+U16 = mybir.dt.uint16
+U8 = mybir.dt.uint8
+FP8X4 = mybir.dt.float8_e4m3fn_x4
+MULT = mybir.AluOpType.mult
+ADD = mybir.AluOpType.add
+SILU = mybir.ActivationFunctionType.Silu
+
+P = 128
+PACK = 4
+K_PASS = P * PACK
+PASSES = K // K_PASS
+M_TILES = N // P
+HALF = S // 2
+LIST_COLS = S // 16
+HALF_COLS = HALF // 16
+
+
+def interleave(copy, dst, src):
+    copy(
+        out=dst.rearrange("p (c i) j -> p c j i", i=4),
+        in_=src.rearrange("p j (c i) -> p c j i", i=4),
+    )
+
+
+def tile_picked_cbn_silu_e_kernel(tc, xT, w1, gamma, beta, offs, cls, out):
+    nc = tc.nc
+    halves = [slice(h * HALF, (h + 1) * HALF) for h in range(2)]
+    list_halves = [slice(h * HALF_COLS, (h + 1) * HALF_COLS) for h in range(2)]
+
+    with ExitStack() as ctx:
+        keep = ctx.enter_context(tc.tile_pool(name="keep", bufs=1))
+        psum = ctx.enter_context(tc.psum_pool(name="psum", bufs=1))
+
+        sample_list = keep.tile([P, LIST_COLS], U16, name="sample_list")
+        class_list = keep.tile([P, LIST_COLS], U16, name="class_list")
+
+        x_rows = xT.rearrange("(g p j) t -> g j p t", g=PASSES, j=PACK)
+        x_plane = [
+            [keep.tile([P, T], F32, name="x_%d_%d" % (g, j)) for j in range(PACK)]
+            for g in range(PASSES)
+        ]
+        w_rows = w1.rearrange("(g p j) m -> g p j m", g=PASSES, j=PACK)
+        w_raw = [keep.tile([P, PACK, N], F32, name="w_raw_%d" % g) for g in range(PASSES)]
+        gamma_table = [keep.tile([P, U], F32, name="gamma_%d" % m) for m in range(M_TILES)]
+        beta_table = [keep.tile([P, U], F32, name="beta_%d" % m) for m in range(M_TILES)]
+
+        nc.sync.dma_start(out=x_plane[0][0][:], in_=x_rows[0, 0])
+        nc.sync.dma_start(out=sample_list[:], in_=offs)
+        nc.sync.dma_start(out=class_list[:], in_=cls)
+        for g in range(PASSES):
+            for j in range(PACK):
+                if (g, j) != (0, 0):
+                    nc.sync.dma_start(out=x_plane[g][j][:], in_=x_rows[g, j])
+        for g in range(PASSES):
+            nc.sync.dma_start(out=w_raw[g][:], in_=w_rows[g])
+        for m in range(M_TILES):
+            nc.sync.dma_start(out=gamma_table[m][:], in_=gamma[m * P : (m + 1) * P, :])
+            nc.sync.dma_start(out=beta_table[m][:], in_=beta[m * P : (m + 1) * P, :])
+
+        x_codes = [keep.tile([P, S], U32, align_bytes=64, name="x_codes_%d" % g) for g in range(PASSES)]
+        x_scales = [keep.tile([P, S], U8, align_bytes=64, name="x_scales_%d" % g) for g in range(PASSES)]
+        for g in range(PASSES):
+            picked = [
+                keep.tile([P, HALF, PACK], BF16, align_bytes=64, name="picked_%d_%d" % (g, h))
+                for h in range(2)
+            ]
+            for j in range(PACK):
+                for h in range(2):
+                    nc.vector.tensor_copy(
+                        out=picked[h][:, :, j],
+                        in_=x_plane[g][j][:].indirect(sample_list[:, list_halves[h]]),
+                    )
+            for h in range(2):
+                nc.vector.quantize_mx(
+                    out=x_codes[g][:, halves[h]].bitcast(FP8X4),
+                    scales=x_scales[g][:, halves[h]],
+                    in_=picked[h][:].rearrange("p s j -> p (s j)"),
+                )
+
+        w_bf = [
+            keep.tile([P, PASSES, P, PACK], BF16, align_bytes=64, name="w_bf_%d" % m)
+            for m in range(M_TILES)
+        ]
+        w_codes = [
+            keep.tile([P, PASSES, P], U32, align_bytes=64, name="w_codes_%d" % m)
+            for m in range(M_TILES)
+        ]
+        w_scales = [
+            keep.tile([P, PASSES, P], U8, align_bytes=64, name="w_scales_%d" % m)
+            for m in range(M_TILES)
+        ]
+        interleave(nc.scalar.copy, w_bf[0][:, 0], w_raw[0][:, :, 0:P])
+        interleave(nc.scalar.copy, w_bf[1][:, 0], w_raw[0][:, :, P:N])
+        interleave(nc.scalar.copy, w_bf[1][:, 1], w_raw[1][:, :, P:N])
+        interleave(nc.vector.tensor_copy, w_bf[0][:, 1], w_raw[1][:, :, 0:P])
+        for g in range(PASSES):
+            nc.vector.quantize_mx(
+                out=w_codes[0][:, g].bitcast(FP8X4),
+                scales=w_scales[0][:, g],
+                in_=w_bf[0][:, g].rearrange("p m j -> p (m j)"),
+            )
+        nc.vector.quantize_mx(
+            out=w_codes[1][:].rearrange("p g m -> p (g m)").bitcast(FP8X4),
+            scales=w_scales[1][:].rearrange("p g m -> p (g m)"),
+            in_=w_bf[1][:].rearrange("p g m j -> p (g m j)"),
+        )
+
+        y_bank = [psum.tile([P, S], F32, name="y_%d" % m) for m in range(M_TILES)]
+        for m in range(M_TILES):
+            for g in range(PASSES):
+                nc.tensor.matmul_mx(
+                    out=y_bank[m][:],
+                    lhsT=w_codes[m][:, g].bitcast(FP8X4),
+                    lhsT_scale=w_scales[m][:, g],
+                    rhs=x_codes[g][:].bitcast(FP8X4),
+                    rhs_scale=x_scales[g][:],
+                    start=(g == 0),
+                    stop=(g == PASSES - 1),
+                )
+
+        def half_tiles(stem):
+            return [keep.tile([P, HALF], F32, name="%s_%d" % (stem, h)) for h in range(2)]
+
+        def finish(m, scaled):
+            shifted = half_tiles("shifted_%d" % m)
+            result = half_tiles("result_%d" % m)
+            for h in range(2):
+                nc.vector.tensor_tensor(
+                    out=shifted[h][:],
+                    in0=beta_table[m][:].indirect(class_list[:, list_halves[h]]),
+                    in1=scaled[h][:],
+                    op=ADD,
+                )
+                nc.scalar.activation(out=result[h][:], in_=shifted[h][:], func=SILU)
+                nc.sync.dma_start(out=out[m * P : (m + 1) * P, halves[h]], in_=result[h][:])
+
+        gamma_picked = half_tiles("gamma_picked")
+        scaled_0 = half_tiles("scaled_0")
+        for h in range(2):
+            nc.vector.tensor_copy(
+                out=gamma_picked[h][:],
+                in_=gamma_table[0][:].indirect(class_list[:, list_halves[h]]),
+            )
+        for h in range(2):
+            nc.vector.tensor_tensor(
+                out=scaled_0[h][:], in0=y_bank[0][:, halves[h]], in1=gamma_picked[h][:], op=MULT
+            )
+        y_1 = half_tiles("y_sbuf_1")
+        for h in range(2):
+            nc.scalar.copy(out=y_1[h][:], in_=y_bank[1][:, halves[h]])
+        finish(0, scaled_0)
+
+        scaled_1 = half_tiles("scaled_1")
+        for h in range(2):
+            nc.vector.tensor_tensor(
+                out=scaled_1[h][:],
+                in0=gamma_table[1][:].indirect(class_list[:, list_halves[h]]),
+                in1=y_1[h][:],
+                op=MULT,
+            )
+        finish(1, scaled_1)

@@ -23,6 +23,7 @@ M_TILES = N // P
 HALF = S // 2
 LIST_COLS = S // 16
 HALF_COLS = HALF // 16
+LAST = 128
 
 
 def interleave(copy, dst, src):
@@ -44,23 +45,25 @@ def tile_picked_cbn_silu_e_kernel(tc, xT, w1, gamma, beta, offs, cls, out):
         sample_list = keep.tile([P, LIST_COLS], U16, name="sample_list")
         class_list = keep.tile([P, LIST_COLS], U16, name="class_list")
 
-        x_rows = xT.rearrange("(g p j) t -> g j p t", g=PASSES, j=PACK)
-        x_plane = [
-            [keep.tile([P, T], F32, name="x_%d_%d" % (g, j)) for j in range(PACK)]
-            for g in range(PASSES)
+        x_rows = xT.rearrange("(g p j) t -> g p j t", g=PASSES, j=PACK)
+        x_loads = [(0, 0, 2), (0, 2, 4), (1, 0, 2), (1, 2, 3), (1, 3, 4)]
+        x_tiles = [
+            keep.tile([P, j1 - j0, T], F32, name="x_%d_%d" % (g, j0)) for g, j0, j1 in x_loads
         ]
+        x_plane = {}
+        for tile, (g, j0, j1) in zip(x_tiles, x_loads):
+            for j in range(j0, j1):
+                x_plane[g, j] = tile[:, j - j0, :]
         w_rows = w1.rearrange("(g p j) m -> g p j m", g=PASSES, j=PACK)
         w_raw = [keep.tile([P, PACK, N], F32, name="w_raw_%d" % g) for g in range(PASSES)]
         gamma_table = [keep.tile([P, U], F32, name="gamma_%d" % m) for m in range(M_TILES)]
         beta_table = [keep.tile([P, U], F32, name="beta_%d" % m) for m in range(M_TILES)]
 
-        nc.sync.dma_start(out=x_plane[0][0][:], in_=x_rows[0, 0])
-        nc.sync.dma_start(out=sample_list[:], in_=offs)
-        nc.sync.dma_start(out=class_list[:], in_=cls)
-        for g in range(PASSES):
-            for j in range(PACK):
-                if (g, j) != (0, 0):
-                    nc.sync.dma_start(out=x_plane[g][j][:], in_=x_rows[g, j])
+        for n, (g, j0, j1) in enumerate(x_loads):
+            nc.sync.dma_start(out=x_tiles[n][:], in_=x_rows[g, :, j0:j1, :])
+            if n == 0:
+                nc.sync.dma_start(out=sample_list[:], in_=offs)
+                nc.sync.dma_start(out=class_list[:], in_=cls)
         for g in range(PASSES):
             nc.sync.dma_start(out=w_raw[g][:], in_=w_rows[g])
         for m in range(M_TILES):
@@ -74,11 +77,19 @@ def tile_picked_cbn_silu_e_kernel(tc, xT, w1, gamma, beta, offs, cls, out):
                 keep.tile([P, HALF, PACK], BF16, align_bytes=64, name="picked_%d_%d" % (g, h))
                 for h in range(2)
             ]
-            for j in range(PACK):
+            for h in range(2):
+                dense = keep.tile([P, 2, HALF], F32, name="dense_%d_%d" % (g, h))
+                for j in range(2):
+                    nc.vector.tensor_copy(
+                        out=dense[:, j, :],
+                        in_=x_plane[g, j].indirect(sample_list[:, list_halves[h]]),
+                    )
+                interleave(nc.scalar.copy, picked[h][:, :, 0:2], dense[:])
+            for j in range(2, PACK):
                 for h in range(2):
                     nc.vector.tensor_copy(
                         out=picked[h][:, :, j],
-                        in_=x_plane[g][j][:].indirect(sample_list[:, list_halves[h]]),
+                        in_=x_plane[g, j].indirect(sample_list[:, list_halves[h]]),
                     )
             for h in range(2):
                 nc.vector.quantize_mx(
@@ -128,44 +139,50 @@ def tile_picked_cbn_silu_e_kernel(tc, xT, w1, gamma, beta, offs, cls, out):
                     stop=(g == PASSES - 1),
                 )
 
-        def half_tiles(stem):
-            return [keep.tile([P, HALF], F32, name="%s_%d" % (stem, h)) for h in range(2)]
+        def piece_tiles(stem, pieces):
+            return [
+                keep.tile([P, c.stop - c.start], F32, name="%s_%d" % (stem, c.start)) for c in pieces
+            ]
 
-        def finish(m, scaled):
-            shifted = half_tiles("shifted_%d" % m)
-            result = half_tiles("result_%d" % m)
-            for h in range(2):
+        def class_offsets(cols):
+            return class_list[:, cols.start // 16 : cols.stop // 16]
+
+        def finish(m, pieces, scaled, store_queues):
+            shifted = piece_tiles("shifted_%d" % m, pieces)
+            result = piece_tiles("result_%d" % m, pieces)
+            for h, cols in enumerate(pieces):
                 nc.vector.tensor_tensor(
                     out=shifted[h][:],
-                    in0=beta_table[m][:].indirect(class_list[:, list_halves[h]]),
+                    in0=beta_table[m][:].indirect(class_offsets(cols)),
                     in1=scaled[h][:],
                     op=ADD,
                 )
                 nc.scalar.activation(out=result[h][:], in_=shifted[h][:], func=SILU)
-                nc.sync.dma_start(out=out[m * P : (m + 1) * P, halves[h]], in_=result[h][:])
+                store_queues[h].dma_start(out=out[m * P : (m + 1) * P, cols], in_=result[h][:])
 
-        gamma_picked = half_tiles("gamma_picked")
-        scaled_0 = half_tiles("scaled_0")
+        gamma_picked = piece_tiles("gamma_picked", halves)
+        scaled_0 = piece_tiles("scaled_0", halves)
         for h in range(2):
             nc.vector.tensor_copy(
                 out=gamma_picked[h][:],
-                in_=gamma_table[0][:].indirect(class_list[:, list_halves[h]]),
+                in_=gamma_table[0][:].indirect(class_offsets(halves[h])),
             )
         for h in range(2):
             nc.vector.tensor_tensor(
                 out=scaled_0[h][:], in0=y_bank[0][:, halves[h]], in1=gamma_picked[h][:], op=MULT
             )
-        y_1 = half_tiles("y_sbuf_1")
-        for h in range(2):
-            nc.scalar.copy(out=y_1[h][:], in_=y_bank[1][:, halves[h]])
-        finish(0, scaled_0)
+        last_pieces = [slice(0, S - LAST), slice(S - LAST, S)]
+        y_1 = piece_tiles("y_sbuf_1", last_pieces)
+        for h, cols in enumerate(last_pieces):
+            nc.scalar.copy(out=y_1[h][:], in_=y_bank[1][:, cols])
+        finish(0, halves, scaled_0, [nc.sync, nc.sync])
 
-        scaled_1 = half_tiles("scaled_1")
-        for h in range(2):
+        scaled_1 = piece_tiles("scaled_1", last_pieces)
+        for h, cols in enumerate(last_pieces):
             nc.vector.tensor_tensor(
                 out=scaled_1[h][:],
-                in0=gamma_table[1][:].indirect(class_list[:, list_halves[h]]),
+                in0=gamma_table[1][:].indirect(class_offsets(cols)),
                 in1=y_1[h][:],
                 op=MULT,
             )
-        finish(1, scaled_1)
+        finish(1, last_pieces, scaled_1, [nc.sync, nc.scalar])

@@ -1,6 +1,7 @@
 from contextlib import ExitStack
 
 import concourse.mybir as mybir
+from concourse.masks import make_identity
 
 K, T, S, N, U = 1024, 2048, 512, 256, 1024
 FLOPS = 2 * K * S * N
@@ -66,9 +67,13 @@ def tile_picked_cbn_silu_e_kernel(tc, xT, w1, gamma, beta, offs, cls, out):
                 nc.sync.dma_start(out=class_list[:], in_=cls)
         for g in range(PASSES):
             nc.sync.dma_start(out=w_raw[g][:], in_=w_rows[g])
-        for m in range(M_TILES):
-            nc.sync.dma_start(out=gamma_table[m][:], in_=gamma[m * P : (m + 1) * P, :])
-            nc.sync.dma_start(out=beta_table[m][:], in_=beta[m * P : (m + 1) * P, :])
+        nc.sync.dma_start(out=beta_table[0][:], in_=beta[0:P, :])
+        nc.sync.dma_start(out=gamma_table[0][:], in_=gamma[0:P, :])
+        nc.sync.dma_start(out=gamma_table[1][:], in_=gamma[P:N, :])
+        nc.sync.dma_start(out=beta_table[1][:], in_=beta[P:N, :])
+
+        identity = keep.tile([P, P], F32, name="identity")
+        make_identity(nc, identity[:])
 
         x_codes = [keep.tile([P, S], U32, align_bytes=64, name="x_codes_%d" % g) for g in range(PASSES)]
         x_scales = [keep.tile([P, S], U8, align_bytes=64, name="x_scales_%d" % g) for g in range(PASSES)]
@@ -126,18 +131,22 @@ def tile_picked_cbn_silu_e_kernel(tc, xT, w1, gamma, beta, offs, cls, out):
             in_=w_bf[1][:].rearrange("p g m j -> p (g m j)"),
         )
 
-        y_bank = [psum.tile([P, S], F32, name="y_%d" % m) for m in range(M_TILES)]
-        for m in range(M_TILES):
+        def product(m, cols):
+            bank = psum.tile([P, cols.stop - cols.start], F32, name="y_%d_%d" % (m, cols.start))
             for g in range(PASSES):
                 nc.tensor.matmul_mx(
-                    out=y_bank[m][:],
+                    out=bank[:],
                     lhsT=w_codes[m][:, g].bitcast(FP8X4),
                     lhsT_scale=w_scales[m][:, g],
-                    rhs=x_codes[g][:].bitcast(FP8X4),
-                    rhs_scale=x_scales[g][:],
+                    rhs=x_codes[g][:, cols].bitcast(FP8X4),
+                    rhs_scale=x_scales[g][:, cols],
                     start=(g == 0),
                     stop=(g == PASSES - 1),
                 )
+            return bank
+
+        y_banks_0 = [product(0, cols) for cols in halves]
+        y_bank_1 = product(1, slice(0, S))
 
         def piece_tiles(stem, pieces):
             return [
@@ -160,22 +169,48 @@ def tile_picked_cbn_silu_e_kernel(tc, xT, w1, gamma, beta, offs, cls, out):
                 nc.scalar.activation(out=result[h][:], in_=shifted[h][:], func=SILU)
                 store_queues[h].dma_start(out=out[m * P : (m + 1) * P, cols], in_=result[h][:])
 
-        gamma_picked = piece_tiles("gamma_picked", halves)
-        scaled_0 = piece_tiles("scaled_0", halves)
+        beta_picked = piece_tiles("beta_picked", halves)
         for h in range(2):
             nc.vector.tensor_copy(
-                out=gamma_picked[h][:],
-                in_=gamma_table[0][:].indirect(class_offsets(halves[h])),
+                out=beta_picked[h][:],
+                in_=beta_table[0][:].indirect(class_offsets(halves[h])),
             )
+        y_0 = piece_tiles("y_sbuf_0", halves)
+        scaled_0 = piece_tiles("scaled_0", halves)
         for h in range(2):
+            nc.scalar.copy(out=y_0[h][:], in_=y_banks_0[h][:])
             nc.vector.tensor_tensor(
-                out=scaled_0[h][:], in0=y_bank[0][:, halves[h]], in1=gamma_picked[h][:], op=MULT
+                out=scaled_0[h][:],
+                in0=gamma_table[0][:].indirect(class_offsets(halves[h])),
+                in1=y_0[h][:],
+                op=MULT,
             )
         last_pieces = [slice(0, S - LAST), slice(S - LAST, S)]
         y_1 = piece_tiles("y_sbuf_1", last_pieces)
         for h, cols in enumerate(last_pieces):
-            nc.scalar.copy(out=y_1[h][:], in_=y_bank[1][:, cols])
-        finish(0, halves, scaled_0, [nc.sync, nc.sync])
+            nc.scalar.copy(out=y_1[h][:], in_=y_bank_1[:, cols])
+        for h, cols in enumerate(halves):
+            summed = psum.tile([P, HALF], F32, name="summed_%d" % h)
+            for c in range(HALF // P):
+                block = slice(c * P, (c + 1) * P)
+                for n, term in enumerate((beta_picked[h], scaled_0[h])):
+                    nc.tensor.matmul(
+                        summed[:, block],
+                        lhsT=term[:, block],
+                        rhs=identity[:],
+                        is_transpose=True,
+                        start=(n == 0),
+                        stop=(n == 1),
+                    )
+            turned = keep.tile([P, HALF], F32, name="turned_%d" % h)
+            nc.scalar.activation(out=turned[:], in_=summed[:], func=SILU)
+            back = psum.tile([P, HALF], F32, name="back_%d" % h)
+            for c in range(HALF // P):
+                block = slice(c * P, (c + 1) * P)
+                nc.tensor.transpose(back[:, block], turned[:, block], identity[:])
+            result_0 = keep.tile([P, HALF], F32, name="result_0_%d" % h)
+            nc.scalar.copy(out=result_0[:], in_=back[:])
+            nc.sync.dma_start(out=out[0:P, cols], in_=result_0[:])
 
         scaled_1 = piece_tiles("scaled_1", last_pieces)
         for h, cols in enumerate(last_pieces):

@@ -72,6 +72,11 @@ def tile_picked_cbn_silu_e_kernel(tc, xT, w1, gamma, beta, offs, cls, out):
         nc.sync.dma_start(out=gamma_table[1][:], in_=gamma[P:N, :])
         nc.sync.dma_start(out=beta_table[1][:], in_=beta[P:N, :])
 
+        warm_in = keep.tile([P, 1], F32, name="warm_in")
+        warm_out = keep.tile([P, 1], F32, name="warm_out")
+        nc.vector.memset(warm_in[:], 0.0)
+        nc.scalar.activation(out=warm_out[:], in_=warm_in[:], func=SILU)
+
         identity = keep.tile([P, P], F32, name="identity")
         make_identity(nc, identity[:])
 
@@ -103,41 +108,30 @@ def tile_picked_cbn_silu_e_kernel(tc, xT, w1, gamma, beta, offs, cls, out):
                     in_=picked[h][:].rearrange("p s j -> p (s j)"),
                 )
 
-        w_bf = [
-            keep.tile([P, PASSES, P, PACK], BF16, align_bytes=64, name="w_bf_%d" % m)
-            for m in range(M_TILES)
-        ]
-        w_codes = [
-            keep.tile([P, PASSES, P], U32, align_bytes=64, name="w_codes_%d" % m)
-            for m in range(M_TILES)
-        ]
-        w_scales = [
-            keep.tile([P, PASSES, P], U8, align_bytes=64, name="w_scales_%d" % m)
-            for m in range(M_TILES)
-        ]
-        interleave(nc.scalar.copy, w_bf[0][:, 0], w_raw[0][:, :, 0:P])
-        interleave(nc.scalar.copy, w_bf[1][:, 0], w_raw[0][:, :, P:N])
-        interleave(nc.scalar.copy, w_bf[1][:, 1], w_raw[1][:, :, P:N])
-        interleave(nc.vector.tensor_copy, w_bf[0][:, 1], w_raw[1][:, :, 0:P])
+        w_codes = {}
+        w_scales = {}
         for g in range(PASSES):
-            nc.vector.quantize_mx(
-                out=w_codes[0][:, g].bitcast(FP8X4),
-                scales=w_scales[0][:, g],
-                in_=w_bf[0][:, g].rearrange("p m j -> p (m j)"),
-            )
-        nc.vector.quantize_mx(
-            out=w_codes[1][:].rearrange("p g m -> p (g m)").bitcast(FP8X4),
-            scales=w_scales[1][:].rearrange("p g m -> p (g m)"),
-            in_=w_bf[1][:].rearrange("p g m j -> p (g m j)"),
-        )
+            for m in range(M_TILES):
+                w_bf = keep.tile([P, P, PACK], BF16, align_bytes=64, name="w_bf_%d_%d" % (g, m))
+                w_codes[g, m] = keep.tile([P, P], U32, align_bytes=64, name="w_codes_%d_%d" % (g, m))
+                w_scales[g, m] = keep.tile([P, P], U8, align_bytes=64, name="w_scales_%d_%d" % (g, m))
+                copy = nc.vector.tensor_copy if (g, m) == (PASSES - 1, 0) else nc.scalar.copy
+                interleave(copy, w_bf[:], w_raw[g][:, :, m * P : (m + 1) * P])
+                nc.vector.quantize_mx(
+                    out=w_codes[g, m][:].bitcast(FP8X4),
+                    scales=w_scales[g, m][:],
+                    in_=w_bf[:].rearrange("p m j -> p (m j)"),
+                )
 
         def product(m, cols):
-            bank = psum.tile([P, cols.stop - cols.start], F32, name="y_%d_%d" % (m, cols.start))
+            bank = psum.tile(
+                [P, cols.stop - cols.start], F32, name="y", tag="bank_%d_%d" % (m, cols.start)
+            )
             for g in range(PASSES):
                 nc.tensor.matmul_mx(
                     out=bank[:],
-                    lhsT=w_codes[m][:, g].bitcast(FP8X4),
-                    lhsT_scale=w_scales[m][:, g],
+                    lhsT=w_codes[g, m][:].bitcast(FP8X4),
+                    lhsT_scale=w_scales[g, m][:],
                     rhs=x_codes[g][:, cols].bitcast(FP8X4),
                     rhs_scale=x_scales[g][:, cols],
                     start=(g == 0),
@@ -190,18 +184,18 @@ def tile_picked_cbn_silu_e_kernel(tc, xT, w1, gamma, beta, offs, cls, out):
         for h, cols in enumerate(last_pieces):
             nc.scalar.copy(out=y_1[h][:], in_=y_bank_1[:, cols])
         for h, cols in enumerate(halves):
-            summed = psum.tile([P, HALF], F32, name="summed_%d" % h)
-            for c in range(HALF // P):
-                block = slice(c * P, (c + 1) * P)
-                for n, term in enumerate((beta_picked[h], scaled_0[h])):
-                    nc.tensor.matmul(
-                        summed[:, block],
-                        lhsT=term[:, block],
-                        rhs=identity[:],
-                        is_transpose=True,
-                        start=(n == 0),
-                        stop=(n == 1),
-                    )
+            summed = psum.tile([P, HALF], F32, name="summed", tag="bank_0_%d" % cols.start)
+            blocks = [slice(c * P, (c + 1) * P) for c in range(HALF // P)]
+            terms = [(term, block) for term in (beta_picked[h], scaled_0[h]) for block in blocks]
+            for n, (term, block) in enumerate(terms):
+                nc.tensor.matmul(
+                    summed[:, block],
+                    lhsT=term[:, block],
+                    rhs=identity[:],
+                    is_transpose=True,
+                    start=(n == 0),
+                    stop=(n == len(terms) - 1),
+                )
             turned = keep.tile([P, HALF], F32, name="turned_%d" % h)
             nc.scalar.activation(out=turned[:], in_=summed[:], func=SILU)
             back = psum.tile([P, HALF], F32, name="back_%d" % h)

@@ -184,26 +184,27 @@ def tile_picked_cbn_silu_e_kernel(tc, xT, w1, gamma, beta, offs, cls, out):
         for h, cols in enumerate(last_pieces):
             nc.scalar.copy(out=y_1[h][:], in_=y_bank_1[:, cols])
         for h, cols in enumerate(halves):
-            summed = psum.tile([P, HALF], F32, name="summed", tag="bank_0_%d" % cols.start)
-            blocks = [slice(c * P, (c + 1) * P) for c in range(HALF // P)]
-            terms = [(term, block) for term in (beta_picked[h], scaled_0[h]) for block in blocks]
-            for n, (term, block) in enumerate(terms):
-                nc.tensor.matmul(
-                    summed[:, block],
-                    lhsT=term[:, block],
-                    rhs=identity[:],
-                    is_transpose=True,
-                    start=(n == 0),
-                    stop=(n == len(terms) - 1),
-                )
-            turned = keep.tile([P, HALF], F32, name="turned_%d" % h)
-            nc.scalar.activation(out=turned[:], in_=summed[:], func=SILU)
-            back = psum.tile([P, HALF], F32, name="back_%d" % h)
-            for c in range(HALF // P):
-                block = slice(c * P, (c + 1) * P)
-                nc.tensor.transpose(back[:, block], turned[:, block], identity[:])
             result_0 = keep.tile([P, HALF], F32, name="result_0_%d" % h)
-            nc.scalar.copy(out=result_0[:], in_=back[:])
+            blocks = [slice(c * P, (c + 1) * P) for c in range(HALF // P)]
+            tags = ["bank_0_%d" % (cols.start + block.start) for block in blocks]
+            summed = [psum.tile([P, P], F32, name="summed", tag=tag) for tag in tags]
+            for n, term in enumerate((beta_picked[h], scaled_0[h])):
+                for c, block in enumerate(blocks):
+                    nc.tensor.matmul(
+                        summed[c][:],
+                        lhsT=term[:, block],
+                        rhs=identity[:],
+                        is_transpose=True,
+                        start=(n == 0),
+                        stop=(n == 1),
+                    )
+            turned = piece_tiles("turned_%d" % h, blocks)
+            for c in range(len(blocks)):
+                nc.scalar.activation(out=turned[c][:], in_=summed[c][:], func=SILU)
+            for c, block in enumerate(blocks):
+                back = psum.tile([P, P], F32, name="back", tag=tags[c])
+                nc.tensor.transpose(back[:], turned[c][:], identity[:])
+                nc.scalar.copy(out=result_0[:, block], in_=back[:])
             nc.sync.dma_start(out=out[0:P, cols], in_=result_0[:])
 
         scaled_1 = piece_tiles("scaled_1", last_pieces)

@@ -56,7 +56,7 @@ def tile_picked_cbn_silu_e_kernel(tc, xT, w1, gamma, beta, offs, cls, out):
             for j in range(j0, j1):
                 x_plane[g, j] = tile[:, j - j0, :]
         w_rows = w1.rearrange("(g p j) m -> g p j m", g=PASSES, j=PACK)
-        w_raw = [keep.tile([P, PACK, N], F32, name="w_raw_%d" % g) for g in range(PASSES)]
+        w_raw = [keep.tile([P, PACK, N], F32, name="w_raw", tag="w_raw_%d" % g) for g in range(PASSES)]
         gamma_table = [keep.tile([P, U], F32, name="gamma_%d" % m) for m in range(M_TILES)]
         beta_table = [keep.tile([P, U], F32, name="beta_%d" % m) for m in range(M_TILES)]
 
@@ -108,20 +108,33 @@ def tile_picked_cbn_silu_e_kernel(tc, xT, w1, gamma, beta, offs, cls, out):
                     in_=picked[h][:].rearrange("p s j -> p (s j)"),
                 )
 
+        quarters = [(g, m) for g in range(PASSES) for m in range(M_TILES)]
+        w_bf = {
+            q: keep.tile([P, P, PACK], BF16, align_bytes=64, name="w_bf", tag="w_bf_%d_%d" % q)
+            for q in quarters
+        }
+        w_scales = {q: keep.tile([P, P], U8, align_bytes=64, name="w_scales_%d_%d" % q) for q in quarters}
         w_codes = {}
-        w_scales = {}
-        for g in range(PASSES):
-            for m in range(M_TILES):
-                w_bf = keep.tile([P, P, PACK], BF16, align_bytes=64, name="w_bf_%d_%d" % (g, m))
-                w_codes[g, m] = keep.tile([P, P], U32, align_bytes=64, name="w_codes_%d_%d" % (g, m))
-                w_scales[g, m] = keep.tile([P, P], U8, align_bytes=64, name="w_scales_%d_%d" % (g, m))
-                copy = nc.vector.tensor_copy if (g, m) == (PASSES - 1, 0) else nc.scalar.copy
-                interleave(copy, w_bf[:], w_raw[g][:, :, m * P : (m + 1) * P])
-                nc.vector.quantize_mx(
-                    out=w_codes[g, m][:].bitcast(FP8X4),
-                    scales=w_scales[g, m][:],
-                    in_=w_bf[:].rearrange("p m j -> p (m j)"),
-                )
+
+        def round_w(copy, g, m):
+            interleave(copy, w_bf[g, m][:], w_raw[g][:, :, m * P : (m + 1) * P])
+
+        def quantize_w(g, m, tag):
+            w_codes[g, m] = keep.tile([P, P], U32, align_bytes=64, name="w_codes", tag=tag)
+            nc.vector.quantize_mx(
+                out=w_codes[g, m][:].bitcast(FP8X4),
+                scales=w_scales[g, m][:],
+                in_=w_bf[g, m][:].rearrange("p m j -> p (m j)"),
+            )
+
+        round_w(nc.scalar.copy, 0, 0)
+        round_w(nc.scalar.copy, 0, 1)
+        quantize_w(0, 0, "w_codes_0_0")
+        round_w(nc.vector.tensor_copy, 1, 0)
+        quantize_w(1, 0, "w_codes_1_0")
+        quantize_w(0, 1, "w_bf_1_0")
+        round_w(nc.scalar.copy, 1, 1)
+        quantize_w(1, 1, "w_codes_1_1")
 
         def product(m, cols):
             bank = psum.tile(
@@ -140,7 +153,7 @@ def tile_picked_cbn_silu_e_kernel(tc, xT, w1, gamma, beta, offs, cls, out):
             return bank
 
         y_banks_0 = [product(0, cols) for cols in halves]
-        y_bank_1 = product(1, slice(0, S))
+        y_banks_1 = [product(1, cols) for cols in halves]
 
         def piece_tiles(stem, pieces):
             return [
@@ -163,26 +176,25 @@ def tile_picked_cbn_silu_e_kernel(tc, xT, w1, gamma, beta, offs, cls, out):
                 nc.scalar.activation(out=result[h][:], in_=shifted[h][:], func=SILU)
                 store_queues[h].dma_start(out=out[m * P : (m + 1) * P, cols], in_=result[h][:])
 
-        beta_picked = piece_tiles("beta_picked", halves)
+        beta_whole = keep.tile([P, S], F32, name="beta_whole", tag="w_raw_1")
+        nc.vector.tensor_copy(out=beta_whole[:], in_=beta_table[0][:].indirect(class_list[:]))
+        y_0 = keep.tile([P, S], F32, name="y_0")
+        scaled_whole = keep.tile([P, S], F32, name="scaled_whole")
         for h in range(2):
-            nc.vector.tensor_copy(
-                out=beta_picked[h][:],
-                in_=beta_table[0][:].indirect(class_offsets(halves[h])),
-            )
-        y_0 = piece_tiles("y_sbuf_0", halves)
-        scaled_0 = piece_tiles("scaled_0", halves)
-        for h in range(2):
-            nc.scalar.copy(out=y_0[h][:], in_=y_banks_0[h][:])
-            nc.vector.tensor_tensor(
-                out=scaled_0[h][:],
-                in0=gamma_table[0][:].indirect(class_offsets(halves[h])),
-                in1=y_0[h][:],
-                op=MULT,
-            )
+            nc.scalar.copy(out=y_0[:, halves[h]], in_=y_banks_0[h][:])
+        nc.vector.tensor_tensor(
+            out=scaled_whole[:],
+            in0=gamma_table[0][:].indirect(class_list[:]),
+            in1=y_0[:],
+            op=MULT,
+        )
+        beta_picked = [beta_whole[:, cols] for cols in halves]
+        scaled_0 = [scaled_whole[:, cols] for cols in halves]
         last_pieces = [slice(0, S - LAST), slice(S - LAST, S)]
-        y_1 = piece_tiles("y_sbuf_1", last_pieces)
-        for h, cols in enumerate(last_pieces):
-            nc.scalar.copy(out=y_1[h][:], in_=y_bank_1[:, cols])
+        y_whole = keep.tile([P, S], F32, name="y_whole")
+        for h, cols in enumerate(halves):
+            nc.scalar.copy(out=y_whole[:, cols], in_=y_banks_1[h][:])
+        y_1 = [y_whole[:, cols] for cols in last_pieces]
         for h, cols in enumerate(halves):
             result_0 = keep.tile([P, HALF], F32, name="result_0_%d" % h)
             blocks = [slice(c * P, (c + 1) * P) for c in range(HALF // P)]

@@ -23,7 +23,6 @@ PASSES = K // K_PASS
 M_TILES = N // P
 HALF = S // 2
 LIST_COLS = S // 16
-HALF_COLS = HALF // 16
 LAST = 128
 
 
@@ -37,7 +36,6 @@ def interleave(copy, dst, src):
 def tile_picked_cbn_silu_e_kernel(tc, xT, w1, gamma, beta, offs, cls, out):
     nc = tc.nc
     halves = [slice(h * HALF, (h + 1) * HALF) for h in range(2)]
-    list_halves = [slice(h * HALF_COLS, (h + 1) * HALF_COLS) for h in range(2)]
 
     with ExitStack() as ctx:
         keep = ctx.enter_context(tc.tile_pool(name="keep", bufs=1))
@@ -82,30 +80,32 @@ def tile_picked_cbn_silu_e_kernel(tc, xT, w1, gamma, beta, offs, cls, out):
 
         x_codes = [keep.tile([P, S], U32, align_bytes=64, name="x_codes_%d" % g) for g in range(PASSES)]
         x_scales = [keep.tile([P, S], U8, align_bytes=64, name="x_scales_%d" % g) for g in range(PASSES)]
+        whole = slice(0, S)
+
+        def sampled(g, j, cols):
+            return x_plane[g, j].indirect(sample_list[:, cols.start // 16 : cols.stop // 16])
+
+        def gather_pair(picked, g, j0, cols):
+            dense = keep.tile([P, 2, cols.stop - cols.start], F32, name="dense_%d_%d" % (g, j0))
+            for j in range(2):
+                nc.vector.tensor_copy(out=dense[:, j, :], in_=sampled(g, j0 + j, cols))
+            interleave(nc.scalar.copy, picked[:, cols, j0 : j0 + 2], dense[:])
+
         for g in range(PASSES):
-            picked = [
-                keep.tile([P, HALF, PACK], BF16, align_bytes=64, name="picked_%d_%d" % (g, h))
-                for h in range(2)
-            ]
-            for h in range(2):
-                dense = keep.tile([P, 2, HALF], F32, name="dense_%d_%d" % (g, h))
-                for j in range(2):
-                    nc.vector.tensor_copy(
-                        out=dense[:, j, :],
-                        in_=x_plane[g, j].indirect(sample_list[:, list_halves[h]]),
-                    )
-                interleave(nc.scalar.copy, picked[h][:, :, 0:2], dense[:])
-            for j in range(2, PACK):
-                for h in range(2):
-                    nc.vector.tensor_copy(
-                        out=picked[h][:, :, j],
-                        in_=x_plane[g, j].indirect(sample_list[:, list_halves[h]]),
-                    )
-            for h in range(2):
+            picked = keep.tile([P, S, PACK], BF16, align_bytes=64, name="picked_%d" % g)
+            gather_pair(picked, g, 0, whole)
+            if g == 0:
+                gather_pair(picked, g, 2, halves[0])
+                stepped = [(2, halves[1]), (3, halves[1])]
+            else:
+                stepped = [(2, whole), (3, halves[0]), (3, halves[1])]
+            for j, cols in stepped:
+                nc.vector.tensor_copy(out=picked[:, cols, j], in_=sampled(g, j, cols))
+            for cols in halves:
                 nc.vector.quantize_mx(
-                    out=x_codes[g][:, halves[h]].bitcast(FP8X4),
-                    scales=x_scales[g][:, halves[h]],
-                    in_=picked[h][:].rearrange("p s j -> p (s j)"),
+                    out=x_codes[g][:, cols].bitcast(FP8X4),
+                    scales=x_scales[g][:, cols],
+                    in_=picked[:, cols, :].rearrange("p s j -> p (s j)"),
                 )
 
         quarters = [(g, m) for g in range(PASSES) for m in range(M_TILES)]
@@ -131,8 +131,8 @@ def tile_picked_cbn_silu_e_kernel(tc, xT, w1, gamma, beta, offs, cls, out):
         round_w(nc.scalar.copy, 0, 1)
         quantize_w(0, 0, "w_codes_0_0")
         round_w(nc.vector.tensor_copy, 1, 0)
+        quantize_w(0, 1, "w_codes_0_1")
         quantize_w(1, 0, "w_codes_1_0")
-        quantize_w(0, 1, "w_bf_1_0")
         round_w(nc.scalar.copy, 1, 1)
         quantize_w(1, 1, "w_codes_1_1")
 
@@ -140,15 +140,16 @@ def tile_picked_cbn_silu_e_kernel(tc, xT, w1, gamma, beta, offs, cls, out):
             bank = psum.tile(
                 [P, cols.stop - cols.start], F32, name="y", tag="bank_%d_%d" % (m, cols.start)
             )
-            for g in range(PASSES):
+            order = list(range(PASSES)) if m == 0 else list(reversed(range(PASSES)))
+            for g in order:
                 nc.tensor.matmul_mx(
                     out=bank[:],
                     lhsT=w_codes[g, m][:].bitcast(FP8X4),
                     lhsT_scale=w_scales[g, m][:],
                     rhs=x_codes[g][:, cols].bitcast(FP8X4),
                     rhs_scale=x_scales[g][:, cols],
-                    start=(g == 0),
-                    stop=(g == PASSES - 1),
+                    start=(g == order[0]),
+                    stop=(g == order[-1]),
                 )
             return bank
 

@@ -23,7 +23,7 @@ PASSES = K // K_PASS
 M_TILES = N // P
 HALF = S // 2
 LIST_COLS = S // 16
-LAST = 128
+LAST = 192
 
 
 def interleave(copy, dst, src):
@@ -62,7 +62,7 @@ def tile_picked_cbn_silu_e_kernel(tc, xT, w1, gamma, beta, offs, cls, out):
             nc.sync.dma_start(out=x_tiles[n][:], in_=x_rows[g, :, j0:j1, :])
             if n == 0:
                 nc.sync.dma_start(out=sample_list[:], in_=offs)
-                nc.sync.dma_start(out=class_list[:], in_=cls)
+        nc.sync.dma_start(out=class_list[:], in_=cls)
         for g in range(PASSES):
             nc.sync.dma_start(out=w_raw[g][:], in_=w_rows[g])
         nc.sync.dma_start(out=beta_table[0][:], in_=beta[0:P, :])

@@ -140,7 +140,7 @@ def tile_picked_cbn_silu_e_kernel(tc, xT, w1, gamma, beta, offs, cls, out):
             bank = psum.tile(
                 [P, cols.stop - cols.start], F32, name="y", tag="bank_%d_%d" % (m, cols.start)
             )
-            order = list(range(PASSES)) if m == 0 else list(reversed(range(PASSES)))
+            order = list(range(PASSES)) if m == 0 or cols.start == 0 else list(reversed(range(PASSES)))
             for g in order:
                 nc.tensor.matmul_mx(
                     out=bank[:],
@@ -179,23 +179,22 @@ def tile_picked_cbn_silu_e_kernel(tc, xT, w1, gamma, beta, offs, cls, out):
 
         beta_whole = keep.tile([P, S], F32, name="beta_whole", tag="w_raw_1")
         nc.vector.tensor_copy(out=beta_whole[:], in_=beta_table[0][:].indirect(class_list[:]))
-        y_0 = keep.tile([P, S], F32, name="y_0")
-        scaled_whole = keep.tile([P, S], F32, name="scaled_whole")
+        y_0 = piece_tiles("y_0", halves)
+        scaled_0 = piece_tiles("scaled_0", halves)
         for h in range(2):
-            nc.scalar.copy(out=y_0[:, halves[h]], in_=y_banks_0[h][:])
-        nc.vector.tensor_tensor(
-            out=scaled_whole[:],
-            in0=gamma_table[0][:].indirect(class_list[:]),
-            in1=y_0[:],
-            op=MULT,
-        )
+            nc.scalar.copy(out=y_0[h][:], in_=y_banks_0[h][:])
+        for h, cols in enumerate(halves):
+            nc.vector.tensor_tensor(
+                out=scaled_0[h][:],
+                in0=gamma_table[0][:].indirect(class_offsets(cols)),
+                in1=y_0[h][:],
+                op=MULT,
+            )
         beta_picked = [beta_whole[:, cols] for cols in halves]
-        scaled_0 = [scaled_whole[:, cols] for cols in halves]
         last_pieces = [slice(0, S - LAST), slice(S - LAST, S)]
         y_whole = keep.tile([P, S], F32, name="y_whole")
         for h, cols in enumerate(halves):
             nc.scalar.copy(out=y_whole[:, cols], in_=y_banks_1[h][:])
-        y_1 = [y_whole[:, cols] for cols in last_pieces]
         for h, cols in enumerate(halves):
             result_0 = keep.tile([P, HALF], F32, name="result_0_%d" % h)
             blocks = [slice(c * P, (c + 1) * P) for c in range(HALF // P)]
@@ -225,7 +224,7 @@ def tile_picked_cbn_silu_e_kernel(tc, xT, w1, gamma, beta, offs, cls, out):
             nc.vector.tensor_tensor(
                 out=scaled_1[h][:],
                 in0=gamma_table[1][:].indirect(class_offsets(cols)),
-                in1=y_1[h][:],
+                in1=y_whole[:, cols],
                 op=MULT,
             )
         finish(1, last_pieces, scaled_1, [nc.sync, nc.scalar])

@@ -23,7 +23,7 @@ PASSES = K // K_PASS
 M_TILES = N // P
 HALF = S // 2
 LIST_COLS = S // 16
-LAST = 192
+LAST = 128
 
 
 def interleave(copy, dst, src):
@@ -140,7 +140,7 @@ def tile_picked_cbn_silu_e_kernel(tc, xT, w1, gamma, beta, offs, cls, out):
             bank = psum.tile(
                 [P, cols.stop - cols.start], F32, name="y", tag="bank_%d_%d" % (m, cols.start)
             )
-            order = list(range(PASSES)) if m == 0 or cols.start == 0 else list(reversed(range(PASSES)))
+            order = list(range(PASSES)) if m == 0 else list(reversed(range(PASSES)))
             for g in order:
                 nc.tensor.matmul_mx(
                     out=bank[:],
@@ -164,19 +164,6 @@ def tile_picked_cbn_silu_e_kernel(tc, xT, w1, gamma, beta, offs, cls, out):
         def class_offsets(cols):
             return class_list[:, cols.start // 16 : cols.stop // 16]
 
-        def finish(m, pieces, scaled, store_queues):
-            shifted = piece_tiles("shifted_%d" % m, pieces)
-            result = piece_tiles("result_%d" % m, pieces)
-            for h, cols in enumerate(pieces):
-                nc.vector.tensor_tensor(
-                    out=shifted[h][:],
-                    in0=beta_table[m][:].indirect(class_offsets(cols)),
-                    in1=scaled[h][:],
-                    op=ADD,
-                )
-                nc.scalar.activation(out=result[h][:], in_=shifted[h][:], func=SILU)
-                store_queues[h].dma_start(out=out[m * P : (m + 1) * P, cols], in_=result[h][:])
-
         beta_whole = keep.tile([P, S], F32, name="beta_whole", tag="w_raw_1")
         nc.vector.tensor_copy(out=beta_whole[:], in_=beta_table[0][:].indirect(class_list[:]))
         y_0 = piece_tiles("y_0", halves)
@@ -191,10 +178,9 @@ def tile_picked_cbn_silu_e_kernel(tc, xT, w1, gamma, beta, offs, cls, out):
                 op=MULT,
             )
         beta_picked = [beta_whole[:, cols] for cols in halves]
-        last_pieces = [slice(0, S - LAST), slice(S - LAST, S)]
-        y_whole = keep.tile([P, S], F32, name="y_whole")
-        for h, cols in enumerate(halves):
-            nc.scalar.copy(out=y_whole[:, cols], in_=y_banks_1[h][:])
+        y_1 = piece_tiles("y_1", halves)
+        for h in range(2):
+            nc.scalar.copy(out=y_1[h][:], in_=y_banks_1[h][:])
         for h, cols in enumerate(halves):
             result_0 = keep.tile([P, HALF], F32, name="result_0_%d" % h)
             blocks = [slice(c * P, (c + 1) * P) for c in range(HALF // P)]
@@ -219,12 +205,25 @@ def tile_picked_cbn_silu_e_kernel(tc, xT, w1, gamma, beta, offs, cls, out):
                 nc.scalar.copy(out=result_0[:, block], in_=back[:])
             nc.sync.dma_start(out=out[0:P, cols], in_=result_0[:])
 
-        scaled_1 = piece_tiles("scaled_1", last_pieces)
-        for h, cols in enumerate(last_pieces):
+        scaled_1 = piece_tiles("scaled_1", halves)
+        for h, cols in enumerate(halves):
             nc.vector.tensor_tensor(
                 out=scaled_1[h][:],
                 in0=gamma_table[1][:].indirect(class_offsets(cols)),
-                in1=y_whole[:, cols],
+                in1=y_1[h][:],
                 op=MULT,
             )
-        finish(1, last_pieces, scaled_1, [nc.sync, nc.scalar])
+        result_1 = piece_tiles("result_1", halves)
+        cuts = [[slice(0, HALF)], [slice(0, HALF - LAST), slice(HALF - LAST, HALF)]]
+        for h, cols in enumerate(halves):
+            for cut in cuts[h]:
+                part = slice(cols.start + cut.start, cols.start + cut.stop)
+                shifted = keep.tile([P, cut.stop - cut.start], F32, name="shifted_%d" % part.start)
+                nc.vector.tensor_tensor(
+                    out=shifted[:],
+                    in0=beta_table[1][:].indirect(class_offsets(part)),
+                    in1=scaled_1[h][:, cut],
+                    op=ADD,
+                )
+                nc.scalar.activation(out=result_1[h][:, cut], in_=shifted[:], func=SILU)
+            (nc.sync, nc.scalar)[h].dma_start(out=out[P:N, cols], in_=result_1[h][:])

@@ -1,7 +1,6 @@
 from contextlib import ExitStack
 
 import concourse.mybir as mybir
-from concourse.masks import make_identity
 
 K, T, S, N, U = 1024, 2048, 512, 256, 1024
 FLOPS = 2 * K * S * N
@@ -15,6 +14,7 @@ FP8X4 = mybir.dt.float8_e4m3fn_x4
 MULT = mybir.AluOpType.mult
 ADD = mybir.AluOpType.add
 SILU = mybir.ActivationFunctionType.Silu
+COPY = mybir.ActivationFunctionType.Copy
 
 P = 128
 PACK = 4
@@ -36,6 +36,13 @@ def interleave(copy, dst, src):
 def tile_picked_cbn_silu_e_kernel(tc, xT, w1, gamma, beta, offs, cls, out):
     nc = tc.nc
     halves = [slice(h * HALF, (h + 1) * HALF) for h in range(2)]
+    whole = slice(0, S)
+
+    def vector_gather(dst, src):
+        nc.vector.tensor_copy(out=dst, in_=src)
+
+    def scalar_gather(dst, src):
+        nc.scalar.activation(out=dst, in_=src, func=COPY)
 
     with ExitStack() as ctx:
         keep = ctx.enter_context(tc.tile_pool(name="keep", bufs=1))
@@ -65,165 +72,133 @@ def tile_picked_cbn_silu_e_kernel(tc, xT, w1, gamma, beta, offs, cls, out):
         nc.sync.dma_start(out=class_list[:], in_=cls)
         for g in range(PASSES):
             nc.sync.dma_start(out=w_raw[g][:], in_=w_rows[g])
-        nc.sync.dma_start(out=beta_table[0][:], in_=beta[0:P, :])
-        nc.sync.dma_start(out=gamma_table[0][:], in_=gamma[0:P, :])
-        nc.sync.dma_start(out=gamma_table[1][:], in_=gamma[P:N, :])
-        nc.sync.dma_start(out=beta_table[1][:], in_=beta[P:N, :])
+        for m in range(M_TILES):
+            nc.sync.dma_start(out=gamma_table[m][:], in_=gamma[m * P : (m + 1) * P, :])
+            nc.sync.dma_start(out=beta_table[m][:], in_=beta[m * P : (m + 1) * P, :])
 
         warm_in = keep.tile([P, 1], F32, name="warm_in")
         warm_out = keep.tile([P, 1], F32, name="warm_out")
         nc.vector.memset(warm_in[:], 0.0)
         nc.scalar.activation(out=warm_out[:], in_=warm_in[:], func=SILU)
 
-        identity = keep.tile([P, P], F32, name="identity")
-        make_identity(nc, identity[:])
-
-        x_codes = [keep.tile([P, S], U32, align_bytes=64, name="x_codes_%d" % g) for g in range(PASSES)]
-        x_scales = [keep.tile([P, S], U8, align_bytes=64, name="x_scales_%d" % g) for g in range(PASSES)]
-        whole = slice(0, S)
-
-        def sampled(g, j, cols):
-            return x_plane[g, j].indirect(sample_list[:, cols.start // 16 : cols.stop // 16])
-
-        def gather_pair(picked, g, j0, cols):
-            dense = keep.tile([P, 2, cols.stop - cols.start], F32, name="dense_%d_%d" % (g, j0))
-            for j in range(2):
-                nc.vector.tensor_copy(out=dense[:, j, :], in_=sampled(g, j0 + j, cols))
-            interleave(nc.scalar.copy, picked[:, cols, j0 : j0 + 2], dense[:])
-
-        for g in range(PASSES):
-            picked = keep.tile([P, S, PACK], BF16, align_bytes=64, name="picked_%d" % g)
-            gather_pair(picked, g, 0, whole)
-            if g == 0:
-                gather_pair(picked, g, 2, halves[0])
-                stepped = [(2, halves[1]), (3, halves[1])]
-            else:
-                stepped = [(2, whole), (3, halves[0]), (3, halves[1])]
-            for j, cols in stepped:
-                nc.vector.tensor_copy(out=picked[:, cols, j], in_=sampled(g, j, cols))
-            for cols in halves:
-                nc.vector.quantize_mx(
-                    out=x_codes[g][:, cols].bitcast(FP8X4),
-                    scales=x_scales[g][:, cols],
-                    in_=picked[:, cols, :].rearrange("p s j -> p (s j)"),
-                )
-
         quarters = [(g, m) for g in range(PASSES) for m in range(M_TILES)]
-        w_bf = {
-            q: keep.tile([P, P, PACK], BF16, align_bytes=64, name="w_bf", tag="w_bf_%d_%d" % q)
-            for q in quarters
-        }
+        w_bf = {q: keep.tile([P, P, PACK], BF16, align_bytes=64, name="w_bf_%d_%d" % q) for q in quarters}
         w_scales = {q: keep.tile([P, P], U8, align_bytes=64, name="w_scales_%d_%d" % q) for q in quarters}
-        w_codes = {}
+        w_codes = {q: keep.tile([P, P], U32, align_bytes=64, name="w_codes_%d_%d" % q) for q in quarters}
 
         def round_w(copy, g, m):
             interleave(copy, w_bf[g, m][:], w_raw[g][:, :, m * P : (m + 1) * P])
 
-        def quantize_w(g, m, tag):
-            w_codes[g, m] = keep.tile([P, P], U32, align_bytes=64, name="w_codes", tag=tag)
+        def quantize_w(g, m):
             nc.vector.quantize_mx(
                 out=w_codes[g, m][:].bitcast(FP8X4),
                 scales=w_scales[g, m][:],
                 in_=w_bf[g, m][:].rearrange("p m j -> p (m j)"),
             )
 
+        x_codes = [keep.tile([P, S], U32, align_bytes=64, name="x_codes_%d" % g) for g in range(PASSES)]
+        x_scales = [keep.tile([P, S], U8, align_bytes=64, name="x_scales_%d" % g) for g in range(PASSES)]
+        dense = [keep.tile([P, PACK, S], F32, name="dense_%d" % g) for g in range(PASSES)]
+        picked = [
+            keep.tile([P, S, PACK], BF16, align_bytes=64, name="picked_%d" % g) for g in range(PASSES)
+        ]
+
+        def sampled(g, j, cols):
+            return x_plane[g, j].indirect(sample_list[:, cols.start // 16 : cols.stop // 16])
+
+        def quantize_x(g, cols):
+            nc.vector.quantize_mx(
+                out=x_codes[g][:, cols].bitcast(FP8X4),
+                scales=x_scales[g][:, cols],
+                in_=picked[g][:, cols, :].rearrange("p s j -> p (s j)"),
+            )
+
+        for j in range(PACK):
+            (vector_gather, scalar_gather)[j % 2](dense[0][:, j, :], sampled(0, j, whole))
+        interleave(nc.vector.tensor_copy, picked[0][:, halves[0], :], dense[0][:, :, halves[0]])
+        interleave(nc.scalar.copy, picked[0][:, halves[1], :], dense[0][:, :, halves[1]])
+        for cols in halves:
+            quantize_x(0, cols)
+
+        vector_gather(dense[1][:, 0, :], sampled(1, 0, whole))
+        scalar_gather(dense[1][:, 1, :], sampled(1, 1, whole))
+        vector_gather(dense[1][:, 2, halves[0]], sampled(1, 2, halves[0]))
+        scalar_gather(dense[1][:, 2, halves[1]], sampled(1, 2, halves[1]))
+        interleave(nc.vector.tensor_copy, picked[1][:, :, 0:3], dense[1][:, 0:3, :])
+        vector_gather(picked[1][:, halves[0], 3], sampled(1, 3, halves[0]))
+        scalar_gather(dense[1][:, 3, halves[1]], sampled(1, 3, halves[1]))
+        quantize_x(1, halves[0])
+        nc.vector.tensor_copy(out=picked[1][:, halves[1], 3], in_=dense[1][:, 3, halves[1]])
+        quantize_x(1, halves[1])
         round_w(nc.scalar.copy, 0, 0)
         round_w(nc.scalar.copy, 0, 1)
-        quantize_w(0, 0, "w_codes_0_0")
+        quantize_w(0, 0)
         round_w(nc.vector.tensor_copy, 1, 0)
-        quantize_w(0, 1, "w_codes_0_1")
-        quantize_w(1, 0, "w_codes_1_0")
+        quantize_w(0, 1)
+        quantize_w(1, 0)
         round_w(nc.scalar.copy, 1, 1)
-        quantize_w(1, 1, "w_codes_1_1")
+        quantize_w(1, 1)
 
-        def product(m, cols):
-            bank = psum.tile(
-                [P, cols.stop - cols.start], F32, name="y", tag="bank_%d_%d" % (m, cols.start)
-            )
+        y_banks = [
+            [psum.tile([P, HALF], F32, name="y_%d_%d" % (m, h)) for h in range(2)] for m in range(M_TILES)
+        ]
+        for m in range(M_TILES):
             order = list(range(PASSES)) if m == 0 else list(reversed(range(PASSES)))
-            for g in order:
-                nc.tensor.matmul_mx(
-                    out=bank[:],
-                    lhsT=w_codes[g, m][:].bitcast(FP8X4),
-                    lhsT_scale=w_scales[g, m][:],
-                    rhs=x_codes[g][:, cols].bitcast(FP8X4),
-                    rhs_scale=x_scales[g][:, cols],
-                    start=(g == order[0]),
-                    stop=(g == order[-1]),
-                )
-            return bank
-
-        y_banks_0 = [product(0, cols) for cols in halves]
-        y_banks_1 = [product(1, cols) for cols in halves]
-
-        def piece_tiles(stem, pieces):
-            return [
-                keep.tile([P, c.stop - c.start], F32, name="%s_%d" % (stem, c.start)) for c in pieces
-            ]
-
-        def class_offsets(cols):
-            return class_list[:, cols.start // 16 : cols.stop // 16]
-
-        beta_whole = keep.tile([P, S], F32, name="beta_whole", tag="w_raw_1")
-        nc.vector.tensor_copy(out=beta_whole[:], in_=beta_table[0][:].indirect(class_list[:]))
-        y_0 = piece_tiles("y_0", halves)
-        scaled_0 = piece_tiles("scaled_0", halves)
-        for h in range(2):
-            nc.scalar.copy(out=y_0[h][:], in_=y_banks_0[h][:])
-        for h, cols in enumerate(halves):
-            nc.vector.tensor_tensor(
-                out=scaled_0[h][:],
-                in0=gamma_table[0][:].indirect(class_offsets(cols)),
-                in1=y_0[h][:],
-                op=MULT,
-            )
-        beta_picked = [beta_whole[:, cols] for cols in halves]
-        y_1 = piece_tiles("y_1", halves)
-        for h in range(2):
-            nc.scalar.copy(out=y_1[h][:], in_=y_banks_1[h][:])
-        for h, cols in enumerate(halves):
-            result_0 = keep.tile([P, HALF], F32, name="result_0_%d" % h)
-            blocks = [slice(c * P, (c + 1) * P) for c in range(HALF // P)]
-            tags = ["bank_0_%d" % (cols.start + block.start) for block in blocks]
-            summed = [psum.tile([P, P], F32, name="summed", tag=tag) for tag in tags]
-            for n, term in enumerate((beta_picked[h], scaled_0[h])):
-                for c, block in enumerate(blocks):
-                    nc.tensor.matmul(
-                        summed[c][:],
-                        lhsT=term[:, block],
-                        rhs=identity[:],
-                        is_transpose=True,
-                        start=(n == 0),
-                        stop=(n == 1),
+            for h, cols in enumerate(halves):
+                for g in order:
+                    nc.tensor.matmul_mx(
+                        out=y_banks[m][h][:],
+                        lhsT=w_codes[g, m][:].bitcast(FP8X4),
+                        lhsT_scale=w_scales[g, m][:],
+                        rhs=x_codes[g][:, cols].bitcast(FP8X4),
+                        rhs_scale=x_scales[g][:, cols],
+                        start=(g == order[0]),
+                        stop=(g == order[-1]),
                     )
-            turned = piece_tiles("turned_%d" % h, blocks)
-            for c in range(len(blocks)):
-                nc.scalar.activation(out=turned[c][:], in_=summed[c][:], func=SILU)
-            for c, block in enumerate(blocks):
-                back = psum.tile([P, P], F32, name="back", tag=tags[c])
-                nc.tensor.transpose(back[:], turned[c][:], identity[:])
-                nc.scalar.copy(out=result_0[:, block], in_=back[:])
-            nc.sync.dma_start(out=out[0:P, cols], in_=result_0[:])
 
-        scaled_1 = piece_tiles("scaled_1", halves)
+        def half_tiles(stem):
+            return [keep.tile([P, HALF], F32, name="%s_%d" % (stem, h)) for h in range(2)]
+
+        def by_class(table, cols):
+            return table[:].indirect(class_list[:, cols.start // 16 : cols.stop // 16])
+
+        gamma_0 = half_tiles("gamma_picked_0")
+        scaled_0 = half_tiles("scaled_0")
+        shifted_0 = half_tiles("shifted_0")
+        vector_gather(gamma_0[0][:], by_class(gamma_table[0], halves[0]))
+        scalar_gather(gamma_0[1][:], by_class(gamma_table[0], halves[1]))
+        for h in range(2):
+            nc.vector.tensor_tensor(out=scaled_0[h][:], in0=y_banks[0][h][:], in1=gamma_0[h][:], op=MULT)
+        y_1 = keep.tile([P, HALF], F32, name="y_1")
+        nc.scalar.copy(out=y_1[:], in_=y_banks[1][0][:])
+        beta_0 = keep.tile([P, HALF], F32, name="beta_picked_0")
+        scalar_gather(beta_0[:], by_class(beta_table[0], halves[1]))
+        nc.vector.tensor_tensor(
+            out=shifted_0[0][:], in0=by_class(beta_table[0], halves[0]), in1=scaled_0[0][:], op=ADD
+        )
+        nc.vector.tensor_tensor(out=shifted_0[1][:], in0=beta_0[:], in1=scaled_0[1][:], op=ADD)
+
+        gamma_1 = keep.tile([P, HALF], F32, name="gamma_picked_1")
+        scaled_1 = half_tiles("scaled_1")
+        scalar_gather(gamma_1[:], by_class(gamma_table[1], halves[1]))
+        nc.vector.tensor_tensor(
+            out=scaled_1[0][:], in0=by_class(gamma_table[1], halves[0]), in1=y_1[:], op=MULT
+        )
+        nc.vector.tensor_tensor(out=scaled_1[1][:], in0=y_banks[1][1][:], in1=gamma_1[:], op=MULT)
+
+        result_0 = keep.tile([P, S], F32, name="result_0", tag="gamma_1")
         for h, cols in enumerate(halves):
-            nc.vector.tensor_tensor(
-                out=scaled_1[h][:],
-                in0=gamma_table[1][:].indirect(class_offsets(cols)),
-                in1=y_1[h][:],
-                op=MULT,
-            )
-        result_1 = piece_tiles("result_1", halves)
+            nc.scalar.activation(out=result_0[:, cols], in_=shifted_0[h][:], func=SILU)
+            nc.sync.dma_start(out=out[0:P, cols], in_=result_0[:, cols])
+
+        result_1 = half_tiles("result_1")
         cuts = [[slice(0, HALF)], [slice(0, HALF - LAST), slice(HALF - LAST, HALF)]]
         for h, cols in enumerate(halves):
             for cut in cuts[h]:
                 part = slice(cols.start + cut.start, cols.start + cut.stop)
-                shifted = keep.tile([P, cut.stop - cut.start], F32, name="shifted_%d" % part.start)
+                shifted = keep.tile([P, cut.stop - cut.start], F32, name="shifted_1_%d" % part.start)
                 nc.vector.tensor_tensor(
-                    out=shifted[:],
-                    in0=beta_table[1][:].indirect(class_offsets(part)),
-                    in1=scaled_1[h][:, cut],
-                    op=ADD,
+                    out=shifted[:], in0=by_class(beta_table[1], part), in1=scaled_1[h][:, cut], op=ADD
                 )
                 nc.scalar.activation(out=result_1[h][:, cut], in_=shifted[:], func=SILU)
             (nc.sync, nc.scalar)[h].dma_start(out=out[P:N, cols], in_=result_1[h][:])

@@ -52,7 +52,7 @@ def tile_picked_cbn_silu_e_kernel(tc, xT, w1, gamma, beta, offs, cls, out):
         class_list = keep.tile([P, LIST_COLS], U16, name="class_list")
 
         x_rows = xT.rearrange("(g p j) t -> g p j t", g=PASSES, j=PACK)
-        x_loads = [(0, 0, 2), (0, 2, 4), (1, 0, 2), (1, 2, 3), (1, 3, 4)]
+        x_loads = [(0, 0, 4), (1, 0, 2), (1, 2, 3), (1, 3, 4)]
         x_tiles = [
             keep.tile([P, j1 - j0, T], F32, name="x_%d_%d" % (g, j0)) for g, j0, j1 in x_loads
         ]

@@ -24,6 +24,7 @@ M_TILES = N // P
 HALF = S // 2
 LIST_COLS = S // 16
 LAST = 128
+STEPPED = 288
 
 
 def interleave(copy, dst, src):
@@ -86,8 +87,8 @@ def tile_picked_cbn_silu_e_kernel(tc, xT, w1, gamma, beta, offs, cls, out):
         w_scales = {q: keep.tile([P, P], U8, align_bytes=64, name="w_scales_%d_%d" % q) for q in quarters}
         w_codes = {q: keep.tile([P, P], U32, align_bytes=64, name="w_codes_%d_%d" % q) for q in quarters}
 
-        def round_w(copy, g, m):
-            interleave(copy, w_bf[g, m][:], w_raw[g][:, :, m * P : (m + 1) * P])
+        def round_w(copy, g, m, cols=slice(0, P)):
+            interleave(copy, w_bf[g, m][:, cols, :], w_raw[g][:, :, m * P + cols.start : m * P + cols.stop])
 
         def quantize_w(g, m):
             nc.vector.quantize_mx(
@@ -125,18 +126,19 @@ def tile_picked_cbn_silu_e_kernel(tc, xT, w1, gamma, beta, offs, cls, out):
         vector_gather(dense[1][:, 2, halves[0]], sampled(1, 2, halves[0]))
         scalar_gather(dense[1][:, 2, halves[1]], sampled(1, 2, halves[1]))
         interleave(nc.vector.tensor_copy, picked[1][:, :, 0:3], dense[1][:, 0:3, :])
-        vector_gather(picked[1][:, halves[0], 3], sampled(1, 3, halves[0]))
-        scalar_gather(dense[1][:, 3, halves[1]], sampled(1, 3, halves[1]))
-        quantize_x(1, halves[0])
-        nc.vector.tensor_copy(out=picked[1][:, halves[1], 3], in_=dense[1][:, 3, halves[1]])
-        quantize_x(1, halves[1])
+        stepped, staged = slice(0, STEPPED), slice(STEPPED, S)
+        vector_gather(picked[1][:, stepped, 3], sampled(1, 3, stepped))
+        scalar_gather(dense[1][:, 3, staged], sampled(1, 3, staged))
+        nc.vector.tensor_copy(out=picked[1][:, staged, 3], in_=dense[1][:, 3, staged])
+        quantize_x(1, whole)
         round_w(nc.scalar.copy, 0, 0)
         round_w(nc.scalar.copy, 0, 1)
         quantize_w(0, 0)
         round_w(nc.vector.tensor_copy, 1, 0)
-        quantize_w(0, 1)
+        round_w(nc.vector.tensor_copy, 1, 1, slice(0, P // 2))
         quantize_w(1, 0)
-        round_w(nc.scalar.copy, 1, 1)
+        quantize_w(0, 1)
+        round_w(nc.scalar.copy, 1, 1, slice(P // 2, P))
         quantize_w(1, 1)
 
         y_banks = [
@@ -189,7 +191,7 @@ def tile_picked_cbn_silu_e_kernel(tc, xT, w1, gamma, beta, offs, cls, out):
         result_0 = keep.tile([P, S], F32, name="result_0", tag="gamma_1")
         for h, cols in enumerate(halves):
             nc.scalar.activation(out=result_0[:, cols], in_=shifted_0[h][:], func=SILU)
-            nc.sync.dma_start(out=out[0:P, cols], in_=result_0[:, cols])
+        nc.sync.dma_start(out=out[0:P, :], in_=result_0[:])
 
         result_1 = half_tiles("result_1")
         cuts = [[slice(0, HALF)], [slice(0, HALF - LAST), slice(HALF - LAST, HALF)]]

@@ -24,7 +24,7 @@ M_TILES = N // P
 HALF = S // 2
 LIST_COLS = S // 16
 LAST = 128
-STEPPED = 288
+QUARTER = S // 4
 
 
 def interleave(copy, dst, src):
@@ -70,7 +70,8 @@ def tile_picked_cbn_silu_e_kernel(tc, xT, w1, gamma, beta, offs, cls, out):
             nc.sync.dma_start(out=x_tiles[n][:], in_=x_rows[g, :, j0:j1, :])
             if n == 0:
                 nc.sync.dma_start(out=sample_list[:], in_=offs)
-        nc.sync.dma_start(out=class_list[:], in_=cls)
+            if n == 2:
+                nc.sync.dma_start(out=class_list[:], in_=cls)
         for g in range(PASSES):
             nc.sync.dma_start(out=w_raw[g][:], in_=w_rows[g])
         for m in range(M_TILES):
@@ -97,40 +98,44 @@ def tile_picked_cbn_silu_e_kernel(tc, xT, w1, gamma, beta, offs, cls, out):
                 in_=w_bf[g, m][:].rearrange("p m j -> p (m j)"),
             )
 
-        x_codes = [keep.tile([P, S], U32, align_bytes=64, name="x_codes_%d" % g) for g in range(PASSES)]
-        x_scales = [keep.tile([P, S], U8, align_bytes=64, name="x_scales_%d" % g) for g in range(PASSES)]
-        dense = [keep.tile([P, PACK, S], F32, name="dense_%d" % g) for g in range(PASSES)]
-        picked = [
-            keep.tile([P, S, PACK], BF16, align_bytes=64, name="picked_%d" % g) for g in range(PASSES)
-        ]
+        pieces = [(g, h) for g in range(PASSES) for h in range(2)]
+        x_scales = {q: keep.tile([P, HALF], U8, align_bytes=64, name="x_scales_%d_%d" % q) for q in pieces}
+        picked = {q: keep.tile([P, HALF, PACK], BF16, align_bytes=64, name="picked_%d_%d" % q) for q in pieces}
+        dense = [keep.tile([P, PACK - g, S], F32, name="dense_%d" % g) for g in range(PASSES)]
+        x_codes = {}
 
         def sampled(g, j, cols):
             return x_plane[g, j].indirect(sample_list[:, cols.start // 16 : cols.stop // 16])
 
-        def quantize_x(g, cols):
+        def quantize_x(g, h):
+            x_codes[g, h] = keep.tile([P, HALF], U32, align_bytes=64, name="x_codes_%d_%d" % (g, h))
             nc.vector.quantize_mx(
-                out=x_codes[g][:, cols].bitcast(FP8X4),
-                scales=x_scales[g][:, cols],
-                in_=picked[g][:, cols, :].rearrange("p s j -> p (s j)"),
+                out=x_codes[g, h][:].bitcast(FP8X4),
+                scales=x_scales[g, h][:],
+                in_=picked[g, h][:].rearrange("p s j -> p (s j)"),
             )
 
         for j in range(PACK):
             (vector_gather, scalar_gather)[j % 2](dense[0][:, j, :], sampled(0, j, whole))
-        interleave(nc.vector.tensor_copy, picked[0][:, halves[0], :], dense[0][:, :, halves[0]])
-        interleave(nc.scalar.copy, picked[0][:, halves[1], :], dense[0][:, :, halves[1]])
-        for cols in halves:
-            quantize_x(0, cols)
+        interleave(nc.vector.tensor_copy, picked[0, 0][:], dense[0][:, :, halves[0]])
+        interleave(nc.scalar.copy, picked[0, 1][:], dense[0][:, :, halves[1]])
+        for h in range(2):
+            quantize_x(0, h)
 
         vector_gather(dense[1][:, 0, :], sampled(1, 0, whole))
         scalar_gather(dense[1][:, 1, :], sampled(1, 1, whole))
         vector_gather(dense[1][:, 2, halves[0]], sampled(1, 2, halves[0]))
         scalar_gather(dense[1][:, 2, halves[1]], sampled(1, 2, halves[1]))
-        interleave(nc.vector.tensor_copy, picked[1][:, :, 0:3], dense[1][:, 0:3, :])
-        stepped, staged = slice(0, STEPPED), slice(STEPPED, S)
-        vector_gather(picked[1][:, stepped, 3], sampled(1, 3, stepped))
-        scalar_gather(dense[1][:, 3, staged], sampled(1, 3, staged))
-        nc.vector.tensor_copy(out=picked[1][:, staged, 3], in_=dense[1][:, 3, staged])
-        quantize_x(1, whole)
+        for h, cols in enumerate(halves):
+            interleave(nc.vector.tensor_copy, picked[1, h][:, :, 0:3], dense[1][:, :, cols])
+        vector_gather(picked[1, 0][:, :, 3], sampled(1, 3, halves[0]))
+        for q, tag in enumerate(("x_codes_1_0", "staged")):
+            within = slice(q * QUARTER, (q + 1) * QUARTER)
+            staged = keep.tile([P, QUARTER], F32, align_bytes=64, name="staged_%d" % q, tag=tag)
+            scalar_gather(staged[:], sampled(1, 3, slice(HALF + within.start, HALF + within.stop)))
+            nc.vector.tensor_copy(out=picked[1, 1][:, within, 3], in_=staged[:])
+        for h in range(2):
+            quantize_x(1, h)
         round_w(nc.scalar.copy, 0, 0)
         round_w(nc.scalar.copy, 0, 1)
         quantize_w(0, 0)
@@ -146,14 +151,14 @@ def tile_picked_cbn_silu_e_kernel(tc, xT, w1, gamma, beta, offs, cls, out):
         ]
         for m in range(M_TILES):
             order = list(range(PASSES)) if m == 0 else list(reversed(range(PASSES)))
-            for h, cols in enumerate(halves):
+            for h in range(2):
                 for g in order:
                     nc.tensor.matmul_mx(
                         out=y_banks[m][h][:],
                         lhsT=w_codes[g, m][:].bitcast(FP8X4),
                         lhsT_scale=w_scales[g, m][:],
-                        rhs=x_codes[g][:, cols].bitcast(FP8X4),
-                        rhs_scale=x_scales[g][:, cols],
+                        rhs=x_codes[g, h][:].bitcast(FP8X4),
+                        rhs_scale=x_scales[g, h][:],
                         start=(g == order[0]),
                         stop=(g == order[-1]),
                     )

@@ -24,6 +24,7 @@ M_TILES = N // P
 HALF = S // 2
 LIST_COLS = S // 16
 LAST = 128
+GAMMA_ON_VECTOR = 192
 QUARTER = S // 4
 
 
@@ -172,18 +173,28 @@ def tile_picked_cbn_silu_e_kernel(tc, xT, w1, gamma, beta, offs, cls, out):
         gamma_0 = half_tiles("gamma_picked_0")
         scaled_0 = half_tiles("scaled_0")
         shifted_0 = half_tiles("shifted_0")
-        vector_gather(gamma_0[0][:], by_class(gamma_table[0], halves[0]))
+        lead, rest = slice(0, GAMMA_ON_VECTOR), slice(GAMMA_ON_VECTOR, HALF)
+        vector_gather(gamma_0[0][:, lead], by_class(gamma_table[0], lead))
+        scalar_gather(gamma_0[0][:, rest], by_class(gamma_table[0], rest))
         scalar_gather(gamma_0[1][:], by_class(gamma_table[0], halves[1]))
         for h in range(2):
             nc.vector.tensor_tensor(out=scaled_0[h][:], in0=y_banks[0][h][:], in1=gamma_0[h][:], op=MULT)
         y_1 = keep.tile([P, HALF], F32, name="y_1")
         nc.scalar.copy(out=y_1[:], in_=y_banks[1][0][:])
-        beta_0 = keep.tile([P, HALF], F32, name="beta_picked_0")
-        scalar_gather(beta_0[:], by_class(beta_table[0], halves[1]))
+        beta_0 = keep.tile([P, QUARTER], F32, name="beta_picked_0")
+        scalar_gather(beta_0[:], by_class(beta_table[0], slice(S - QUARTER, S)))
         nc.vector.tensor_tensor(
             out=shifted_0[0][:], in0=by_class(beta_table[0], halves[0]), in1=scaled_0[0][:], op=ADD
         )
-        nc.vector.tensor_tensor(out=shifted_0[1][:], in0=beta_0[:], in1=scaled_0[1][:], op=ADD)
+        nc.vector.tensor_tensor(
+            out=shifted_0[1][:, 0:QUARTER],
+            in0=by_class(beta_table[0], slice(HALF, S - QUARTER)),
+            in1=scaled_0[1][:, 0:QUARTER],
+            op=ADD,
+        )
+        nc.vector.tensor_tensor(
+            out=shifted_0[1][:, QUARTER:HALF], in0=beta_0[:], in1=scaled_0[1][:, QUARTER:HALF], op=ADD
+        )
 
         gamma_1 = keep.tile([P, HALF], F32, name="gamma_picked_1")
         scaled_1 = half_tiles("scaled_1")

@@ -141,10 +141,9 @@ def tile_picked_cbn_silu_e_kernel(tc, xT, w1, gamma, beta, offs, cls, out):
         round_w(nc.scalar.copy, 0, 1)
         quantize_w(0, 0)
         round_w(nc.vector.tensor_copy, 1, 0)
-        round_w(nc.vector.tensor_copy, 1, 1, slice(0, P // 2))
-        quantize_w(1, 0)
         quantize_w(0, 1)
-        round_w(nc.scalar.copy, 1, 1, slice(P // 2, P))
+        quantize_w(1, 0)
+        round_w(nc.scalar.copy, 1, 1)
         quantize_w(1, 1)
 
         y_banks = [

@@ -71,10 +71,9 @@ def tile_picked_cbn_silu_e_kernel(tc, xT, w1, gamma, beta, offs, cls, out):
             nc.sync.dma_start(out=x_tiles[n][:], in_=x_rows[g, :, j0:j1, :])
             if n == 0:
                 nc.sync.dma_start(out=sample_list[:], in_=offs)
-            if n == 2:
-                nc.sync.dma_start(out=class_list[:], in_=cls)
         for g in range(PASSES):
             nc.sync.dma_start(out=w_raw[g][:], in_=w_rows[g])
+        nc.sync.dma_start(out=class_list[:], in_=cls)
         for m in range(M_TILES):
             nc.sync.dma_start(out=gamma_table[m][:], in_=gamma[m * P : (m + 1) * P, :])
             nc.sync.dma_start(out=beta_table[m][:], in_=beta[m * P : (m + 1) * P, :])
@@ -178,7 +177,7 @@ def tile_picked_cbn_silu_e_kernel(tc, xT, w1, gamma, beta, offs, cls, out):
         scalar_gather(gamma_0[1][:], by_class(gamma_table[0], halves[1]))
         for h in range(2):
             nc.vector.tensor_tensor(out=scaled_0[h][:], in0=y_banks[0][h][:], in1=gamma_0[h][:], op=MULT)
-        y_1 = keep.tile([P, HALF], F32, name="y_1")
+        y_1 = keep.tile([P, HALF], F32, name="y_1", tag="gamma_picked_0_0")
         nc.scalar.copy(out=y_1[:], in_=y_banks[1][0][:])
         beta_0 = keep.tile([P, QUARTER], F32, name="beta_picked_0")
         scalar_gather(beta_0[:], by_class(beta_table[0], slice(S - QUARTER, S)))

@@ -26,6 +26,7 @@ LIST_COLS = S // 16
 LAST = 128
 GAMMA_ON_VECTOR = 192
 QUARTER = S // 4
+BURST = 256
 
 
 def interleave(copy, dst, src):
@@ -56,16 +57,16 @@ def tile_picked_cbn_silu_e_kernel(tc, xT, w1, gamma, beta, offs, cls, out):
         x_rows = xT.rearrange("(g p j) t -> g p j t", g=PASSES, j=PACK)
         x_loads = [(0, 0, 4), (1, 0, 2), (1, 2, 3), (1, 3, 4)]
         x_tiles = [
-            keep.tile([P, j1 - j0, T], F32, name="x_%d_%d" % (g, j0)) for g, j0, j1 in x_loads
+            keep.tile([P, j1 - j0, T], F32, align_bytes=BURST, name="x_%d_%d" % (g, j0)) for g, j0, j1 in x_loads
         ]
         x_plane = {}
         for tile, (g, j0, j1) in zip(x_tiles, x_loads):
             for j in range(j0, j1):
                 x_plane[g, j] = tile[:, j - j0, :]
         w_rows = w1.rearrange("(g p j) m -> g p j m", g=PASSES, j=PACK)
-        w_raw = [keep.tile([P, PACK, N], F32, name="w_raw", tag="w_raw_%d" % g) for g in range(PASSES)]
-        gamma_table = [keep.tile([P, U], F32, name="gamma_%d" % m) for m in range(M_TILES)]
-        beta_table = [keep.tile([P, U], F32, name="beta_%d" % m) for m in range(M_TILES)]
+        w_raw = [keep.tile([P, PACK, N], F32, align_bytes=BURST, name="w_raw_%d" % g) for g in range(PASSES)]
+        gamma_table = [keep.tile([P, U], F32, align_bytes=BURST, name="gamma_%d" % m) for m in range(M_TILES)]
+        beta_table = [keep.tile([P, U], F32, align_bytes=BURST, name="beta_%d" % m) for m in range(M_TILES)]
 
         for n, (g, j0, j1) in enumerate(x_loads):
             nc.sync.dma_start(out=x_tiles[n][:], in_=x_rows[g, :, j0:j1, :])
@@ -202,12 +203,12 @@ def tile_picked_cbn_silu_e_kernel(tc, xT, w1, gamma, beta, offs, cls, out):
         )
         nc.vector.tensor_tensor(out=scaled_1[1][:], in0=y_banks[1][1][:], in1=gamma_1[:], op=MULT)
 
-        result_0 = keep.tile([P, S], F32, name="result_0", tag="gamma_1")
+        result_0 = keep.tile([P, S], F32, align_bytes=BURST, name="result_0", tag="gamma_1")
         for h, cols in enumerate(halves):
             nc.scalar.activation(out=result_0[:, cols], in_=shifted_0[h][:], func=SILU)
         nc.sync.dma_start(out=out[0:P, :], in_=result_0[:])
 
-        result_1 = half_tiles("result_1")
+        result_1 = [keep.tile([P, HALF], F32, align_bytes=BURST, name="result_1_%d" % h) for h in range(2)]
         cuts = [[slice(0, HALF)], [slice(0, HALF - LAST), slice(HALF - LAST, HALF)]]
         for h, cols in enumerate(halves):
             for cut in cuts[h]:

@@ -23,7 +23,7 @@ PASSES = K // K_PASS
 M_TILES = N // P
 HALF = S // 2
 LIST_COLS = S // 16
-LAST = 128
+LAST = 64
 GAMMA_ON_VECTOR = 192
 QUARTER = S // 4
 BURST = 256

@@ -24,7 +24,7 @@ M_TILES = N // P
 HALF = S // 2
 LIST_COLS = S // 16
 LAST = 64
-GAMMA_ON_VECTOR = 192
+GAMMA_ON_VECTOR = (128, 128)
 QUARTER = S // 4
 BURST = 256
 
@@ -150,8 +150,8 @@ def tile_picked_cbn_silu_e_kernel(tc, xT, w1, gamma, beta, offs, cls, out):
             [psum.tile([P, HALF], F32, name="y_%d_%d" % (m, h)) for h in range(2)] for m in range(M_TILES)
         ]
         for m in range(M_TILES):
-            order = list(range(PASSES)) if m == 0 else list(reversed(range(PASSES)))
             for h in range(2):
+                order = list(range(PASSES)) if (m, h) != (1, 1) else list(reversed(range(PASSES)))
                 for g in order:
                     nc.tensor.matmul_mx(
                         out=y_banks[m][h][:],
@@ -172,10 +172,10 @@ def tile_picked_cbn_silu_e_kernel(tc, xT, w1, gamma, beta, offs, cls, out):
         gamma_0 = half_tiles("gamma_picked_0")
         scaled_0 = half_tiles("scaled_0")
         shifted_0 = half_tiles("shifted_0")
-        lead, rest = slice(0, GAMMA_ON_VECTOR), slice(GAMMA_ON_VECTOR, HALF)
-        vector_gather(gamma_0[0][:, lead], by_class(gamma_table[0], lead))
-        scalar_gather(gamma_0[0][:, rest], by_class(gamma_table[0], rest))
-        scalar_gather(gamma_0[1][:], by_class(gamma_table[0], halves[1]))
+        for h, share in enumerate(GAMMA_ON_VECTOR):
+            first = h * HALF
+            vector_gather(gamma_0[h][:, 0:share], by_class(gamma_table[0], slice(first, first + share)))
+            scalar_gather(gamma_0[h][:, share:HALF], by_class(gamma_table[0], slice(first + share, first + HALF)))
         for h in range(2):
             nc.vector.tensor_tensor(out=scaled_0[h][:], in0=y_banks[0][h][:], in1=gamma_0[h][:], op=MULT)
         y_1 = keep.tile([P, HALF], F32, name="y_1", tag="gamma_picked_0_0")

@@ -164,26 +164,28 @@ def tile_picked_cbn_silu_e_kernel(tc, xT, w1, gamma, beta, offs, cls, out):
                     )
 
         def half_tiles(stem):
-            return [keep.tile([P, HALF], F32, name="%s_%d" % (stem, h)) for h in range(2)]
+            return [keep.tile([P, HALF], F32, align_bytes=BURST, name="%s_%d" % (stem, h)) for h in range(2)]
 
         def by_class(table, cols):
             return table[:].indirect(class_list[:, cols.start // 16 : cols.stop // 16])
 
         gamma_0 = half_tiles("gamma_picked_0")
         scaled_0 = half_tiles("scaled_0")
-        shifted_0 = half_tiles("shifted_0")
+        shifted_row = keep.tile([P, S], F32, name="shifted_0")
+        shifted_0 = [shifted_row[:, cols] for cols in halves]
         for h, share in enumerate(GAMMA_ON_VECTOR):
             first = h * HALF
             vector_gather(gamma_0[h][:, 0:share], by_class(gamma_table[0], slice(first, first + share)))
             scalar_gather(gamma_0[h][:, share:HALF], by_class(gamma_table[0], slice(first + share, first + HALF)))
         for h in range(2):
             nc.vector.tensor_tensor(out=scaled_0[h][:], in0=y_banks[0][h][:], in1=gamma_0[h][:], op=MULT)
-        y_1 = keep.tile([P, HALF], F32, name="y_1", tag="gamma_picked_0_0")
-        nc.scalar.copy(out=y_1[:], in_=y_banks[1][0][:])
+        shared_row = keep.tile([P, S + QUARTER], F32, align_bytes=BURST, name="shared_row", tag="gamma_picked_0_0")
+        y_1 = shared_row[:, S - QUARTER : S + QUARTER]
+        nc.scalar.copy(out=y_1, in_=y_banks[1][0][:])
         beta_0 = keep.tile([P, QUARTER], F32, name="beta_picked_0")
         scalar_gather(beta_0[:], by_class(beta_table[0], slice(S - QUARTER, S)))
         nc.vector.tensor_tensor(
-            out=shifted_0[0][:], in0=by_class(beta_table[0], halves[0]), in1=scaled_0[0][:], op=ADD
+            out=shifted_0[0], in0=by_class(beta_table[0], halves[0]), in1=scaled_0[0][:], op=ADD
         )
         nc.vector.tensor_tensor(
             out=shifted_0[1][:, 0:QUARTER],
@@ -198,15 +200,15 @@ def tile_picked_cbn_silu_e_kernel(tc, xT, w1, gamma, beta, offs, cls, out):
         gamma_1 = keep.tile([P, HALF], F32, name="gamma_picked_1")
         scaled_1 = half_tiles("scaled_1")
         scalar_gather(gamma_1[:], by_class(gamma_table[1], halves[1]))
-        nc.vector.tensor_tensor(
-            out=scaled_1[0][:], in0=by_class(gamma_table[1], halves[0]), in1=y_1[:], op=MULT
-        )
+        for cols in (slice(0, QUARTER), slice(QUARTER, HALF)):
+            nc.vector.tensor_tensor(
+                out=scaled_1[0][:, cols], in0=by_class(gamma_table[1], cols), in1=y_1[:, cols], op=MULT
+            )
         nc.vector.tensor_tensor(out=scaled_1[1][:], in0=y_banks[1][1][:], in1=gamma_1[:], op=MULT)
 
-        result_0 = keep.tile([P, S], F32, align_bytes=BURST, name="result_0", tag="gamma_1")
-        for h, cols in enumerate(halves):
-            nc.scalar.activation(out=result_0[:, cols], in_=shifted_0[h][:], func=SILU)
-        nc.sync.dma_start(out=out[0:P, :], in_=result_0[:])
+        result_0 = shared_row[:, 0:S]
+        nc.scalar.activation(out=result_0, in_=shifted_row[:], func=SILU)
+        nc.sync.dma_start(out=out[0:P, :], in_=result_0)
 
         result_1 = [keep.tile([P, HALF], F32, align_bytes=BURST, name="result_1_%d" % h) for h in range(2)]
         cuts = [[slice(0, HALF)], [slice(0, HALF - LAST), slice(HALF - LAST, HALF)]]

@@ -23,7 +23,6 @@ PASSES = K // K_PASS
 M_TILES = N // P
 HALF = S // 2
 LIST_COLS = S // 16
-LAST = 64
 GAMMA_ON_VECTOR = (128, 128)
 QUARTER = S // 4
 BURST = 256
@@ -81,7 +80,7 @@ def tile_picked_cbn_silu_e_kernel(tc, xT, w1, gamma, beta, offs, cls, out):
 
         warm_in = keep.tile([P, 1], F32, name="warm_in")
         warm_out = keep.tile([P, 1], F32, name="warm_out")
-        nc.vector.memset(warm_in[:], 0.0)
+        nc.gpsimd.memset(warm_in[:], 0.0)
         nc.scalar.activation(out=warm_out[:], in_=warm_in[:], func=SILU)
 
         quarters = [(g, m) for g in range(PASSES) for m in range(M_TILES)]
@@ -210,14 +209,23 @@ def tile_picked_cbn_silu_e_kernel(tc, xT, w1, gamma, beta, offs, cls, out):
         nc.scalar.activation(out=result_0, in_=shifted_row[:], func=SILU)
         nc.sync.dma_start(out=out[0:P, :], in_=result_0)
 
-        result_1 = [keep.tile([P, HALF], F32, align_bytes=BURST, name="result_1_%d" % h) for h in range(2)]
-        cuts = [[slice(0, HALF)], [slice(0, HALF - LAST), slice(HALF - LAST, HALF)]]
-        for h, cols in enumerate(halves):
-            for cut in cuts[h]:
-                part = slice(cols.start + cut.start, cols.start + cut.stop)
-                shifted = keep.tile([P, cut.stop - cut.start], F32, name="shifted_1_%d" % part.start)
-                nc.vector.tensor_tensor(
-                    out=shifted[:], in0=by_class(beta_table[1], part), in1=scaled_1[h][:, cut], op=ADD
-                )
-                nc.scalar.activation(out=result_1[h][:, cut], in_=shifted[:], func=SILU)
-            (nc.sync, nc.scalar)[h].dma_start(out=out[P:N, cols], in_=result_1[h][:])
+        result_1 = half_tiles("result_1")
+        shifted_1 = half_tiles("shifted_1")
+        beta_1 = keep.tile([P, QUARTER], F32, name="beta_picked_1")
+        scalar_gather(beta_1[:], by_class(beta_table[1], slice(S - QUARTER, S)))
+        nc.vector.tensor_tensor(
+            out=shifted_1[0][:], in0=by_class(beta_table[1], halves[0]), in1=scaled_1[0][:], op=ADD
+        )
+        nc.scalar.activation(out=result_1[0][:], in_=shifted_1[0][:], func=SILU)
+        nc.sync.dma_start(out=out[P:N, halves[0]], in_=result_1[0][:])
+        third, fourth = slice(0, QUARTER), slice(QUARTER, HALF)
+        nc.vector.tensor_tensor(
+            out=shifted_1[1][:, third],
+            in0=by_class(beta_table[1], slice(HALF, S - QUARTER)),
+            in1=scaled_1[1][:, third],
+            op=ADD,
+        )
+        nc.vector.tensor_tensor(out=shifted_1[1][:, fourth], in0=beta_1[:], in1=scaled_1[1][:, fourth], op=ADD)
+        for cols in (third, fourth):
+            nc.scalar.activation(out=result_1[1][:, cols], in_=shifted_1[1][:, cols], func=SILU)
+        nc.scalar.dma_start(out=out[P:N, halves[1]], in_=result_1[1][:])

@@ -126,8 +126,8 @@ def tile_picked_cbn_silu_e_kernel(tc, xT, w1, gamma, beta, offs, cls, out):
         scalar_gather(dense[1][:, 1, :], sampled(1, 1, whole))
         vector_gather(dense[1][:, 2, halves[0]], sampled(1, 2, halves[0]))
         scalar_gather(dense[1][:, 2, halves[1]], sampled(1, 2, halves[1]))
-        for h, cols in enumerate(halves):
-            interleave(nc.vector.tensor_copy, picked[1, h][:, :, 0:3], dense[1][:, :, cols])
+        for h, copy in enumerate((nc.vector.tensor_copy, nc.scalar.copy)):
+            interleave(copy, picked[1, h][:, :, 0:3], dense[1][:, :, halves[h]])
         vector_gather(picked[1, 0][:, :, 3], sampled(1, 3, halves[0]))
         for q, tag in enumerate(("x_codes_1_0", "staged")):
             within = slice(q * QUARTER, (q + 1) * QUARTER)

@@ -53,22 +53,22 @@ def tile_picked_cbn_silu_e_kernel(tc, xT, w1, gamma, beta, offs, cls, out):
         sample_list = keep.tile([P, LIST_COLS], U16, name="sample_list")
         class_list = keep.tile([P, LIST_COLS], U16, name="class_list")
 
-        x_rows = xT.rearrange("(g p j) t -> g p j t", g=PASSES, j=PACK)
+        x_rows = xT.rearrange("(g p j) t -> g p (j t)", g=PASSES, j=PACK)
         x_loads = [(0, 0, 4), (1, 0, 2), (1, 2, 3), (1, 3, 4)]
         x_tiles = [
-            keep.tile([P, j1 - j0, T], F32, align_bytes=BURST, name="x_%d_%d" % (g, j0)) for g, j0, j1 in x_loads
+            keep.tile([P, (j1 - j0) * T], F32, align_bytes=BURST, name="x_%d_%d" % (g, j0)) for g, j0, j1 in x_loads
         ]
         x_plane = {}
         for tile, (g, j0, j1) in zip(x_tiles, x_loads):
             for j in range(j0, j1):
-                x_plane[g, j] = tile[:, j - j0, :]
+                x_plane[g, j] = tile[:, (j - j0) * T : (j - j0 + 1) * T]
         w_rows = w1.rearrange("(g p j) m -> g p j m", g=PASSES, j=PACK)
         w_raw = [keep.tile([P, PACK, N], F32, align_bytes=BURST, name="w_raw_%d" % g) for g in range(PASSES)]
         gamma_table = [keep.tile([P, U], F32, align_bytes=BURST, name="gamma_%d" % m) for m in range(M_TILES)]
         beta_table = [keep.tile([P, U], F32, align_bytes=BURST, name="beta_%d" % m) for m in range(M_TILES)]
 
         for n, (g, j0, j1) in enumerate(x_loads):
-            nc.sync.dma_start(out=x_tiles[n][:], in_=x_rows[g, :, j0:j1, :])
+            nc.sync.dma_start(out=x_tiles[n][:], in_=x_rows[g, :, j0 * T : j1 * T])
             if n == 0:
                 nc.sync.dma_start(out=sample_list[:], in_=offs)
         for g in range(PASSES):
@@ -129,12 +129,8 @@ def tile_picked_cbn_silu_e_kernel(tc, xT, w1, gamma, beta, offs, cls, out):
         for h, copy in enumerate((nc.vector.tensor_copy, nc.scalar.copy)):
             interleave(copy, picked[1, h][:, :, 0:3], dense[1][:, :, halves[h]])
         vector_gather(picked[1, 0][:, :, 3], sampled(1, 3, halves[0]))
-        for q, tag in enumerate(("x_codes_1_0", "staged")):
-            within = slice(q * QUARTER, (q + 1) * QUARTER)
-            staged = keep.tile([P, QUARTER], F32, align_bytes=64, name="staged_%d" % q, tag=tag)
-            scalar_gather(staged[:], sampled(1, 3, slice(HALF + within.start, HALF + within.stop)))
-            nc.vector.tensor_copy(out=picked[1, 1][:, within, 3], in_=staged[:])
-        for h in range(2):
+        scalar_gather(picked[1, 1][:, :, 3], sampled(1, 3, halves[1]))
+        for h in (1, 0):
             quantize_x(1, h)
         round_w(nc.scalar.copy, 0, 0)
         round_w(nc.scalar.copy, 0, 1)

@@ -26,6 +26,8 @@ LIST_COLS = S // 16
 GAMMA_ON_VECTOR = (128, 128)
 QUARTER = S // 4
 BURST = 256
+LEAD = 64
+BETA_ON_SCALAR = 192
 
 
 def interleave(copy, dst, src):
@@ -165,43 +167,39 @@ def tile_picked_cbn_silu_e_kernel(tc, xT, w1, gamma, beta, offs, cls, out):
             return table[:].indirect(class_list[:, cols.start // 16 : cols.stop // 16])
 
         gamma_0 = half_tiles("gamma_picked_0")
-        scaled_0 = half_tiles("scaled_0")
+        copied = slice(S - LEAD, S - LEAD + HALF)
+        wide_row = keep.tile([P, copied.stop - LEAD + S], F32, align_bytes=BURST, name="wide_row")
+        scaled_row = wide_row[:, copied.stop - LEAD :]
+        scaled_0 = [scaled_row[:, cols] for cols in halves]
         shifted_row = keep.tile([P, S], F32, name="shifted_0")
-        shifted_0 = [shifted_row[:, cols] for cols in halves]
         for h, share in enumerate(GAMMA_ON_VECTOR):
             first = h * HALF
             vector_gather(gamma_0[h][:, 0:share], by_class(gamma_table[0], slice(first, first + share)))
             scalar_gather(gamma_0[h][:, share:HALF], by_class(gamma_table[0], slice(first + share, first + HALF)))
         for h in range(2):
-            nc.vector.tensor_tensor(out=scaled_0[h][:], in0=y_banks[0][h][:], in1=gamma_0[h][:], op=MULT)
-        shared_row = keep.tile([P, S + QUARTER], F32, align_bytes=BURST, name="shared_row", tag="gamma_picked_0_0")
-        y_1 = shared_row[:, S - QUARTER : S + QUARTER]
-        nc.scalar.copy(out=y_1, in_=y_banks[1][0][:])
-        beta_0 = keep.tile([P, QUARTER], F32, name="beta_picked_0")
-        scalar_gather(beta_0[:], by_class(beta_table[0], slice(S - QUARTER, S)))
-        nc.vector.tensor_tensor(
-            out=shifted_0[0], in0=by_class(beta_table[0], halves[0]), in1=scaled_0[0][:], op=ADD
-        )
-        nc.vector.tensor_tensor(
-            out=shifted_0[1][:, 0:QUARTER],
-            in0=by_class(beta_table[0], slice(HALF, S - QUARTER)),
-            in1=scaled_0[1][:, 0:QUARTER],
-            op=ADD,
-        )
-        nc.vector.tensor_tensor(
-            out=shifted_0[1][:, QUARTER:HALF], in0=beta_0[:], in1=scaled_0[1][:, QUARTER:HALF], op=ADD
-        )
+            nc.vector.tensor_tensor(out=scaled_0[h], in0=y_banks[0][h][:], in1=gamma_0[h][:], op=MULT)
+        shared = slice(S - BETA_ON_SCALAR, S)
+        beta_0 = keep.tile([P, BETA_ON_SCALAR], F32, name="beta_picked_0")
+        scalar_gather(beta_0[:], by_class(beta_table[0], shared))
+        y_1 = wide_row[:, copied]
+        for cols in (slice(0, LEAD), slice(LEAD, shared.start)):
+            nc.vector.tensor_tensor(
+                out=shifted_row[:, cols], in0=by_class(beta_table[0], cols), in1=scaled_row[:, cols], op=ADD
+            )
+            if cols.start == 0:
+                nc.scalar.copy(out=y_1, in_=y_banks[1][0][:])
+        nc.vector.tensor_tensor(out=shifted_row[:, shared], in0=beta_0[:], in1=scaled_row[:, shared], op=ADD)
 
         gamma_1 = keep.tile([P, HALF], F32, name="gamma_picked_1")
         scaled_1 = half_tiles("scaled_1")
         scalar_gather(gamma_1[:], by_class(gamma_table[1], halves[1]))
-        for cols in (slice(0, QUARTER), slice(QUARTER, HALF)):
+        for cols in (slice(0, LEAD), slice(LEAD, HALF)):
             nc.vector.tensor_tensor(
                 out=scaled_1[0][:, cols], in0=by_class(gamma_table[1], cols), in1=y_1[:, cols], op=MULT
             )
         nc.vector.tensor_tensor(out=scaled_1[1][:], in0=y_banks[1][1][:], in1=gamma_1[:], op=MULT)
 
-        result_0 = shared_row[:, 0:S]
+        result_0 = wide_row[:, 0:S]
         nc.scalar.activation(out=result_0, in_=shifted_row[:], func=SILU)
         nc.sync.dma_start(out=out[0:P, :], in_=result_0)
 

from contextlib import ExitStack

import concourse.mybir as mybir

K, T, S, N, U = 1024, 2048, 512, 256, 1024
FLOPS = 2 * K * S * N

F32 = mybir.dt.float32
BF16 = mybir.dt.bfloat16
U32 = mybir.dt.uint32
U16 = mybir.dt.uint16
U8 = mybir.dt.uint8
FP8X4 = mybir.dt.float8_e4m3fn_x4
MULT = mybir.AluOpType.mult
ADD = mybir.AluOpType.add
SILU = mybir.ActivationFunctionType.Silu
COPY = mybir.ActivationFunctionType.Copy

P = 128
PACK = 4
K_PASS = P * PACK
PASSES = K // K_PASS
M_TILES = N // P
HALF = S // 2
LIST_COLS = S // 16
GAMMA_ON_VECTOR = (128, 128)
QUARTER = S // 4
BURST = 256
LEAD = 64
BETA_ON_SCALAR = 192


def interleave(copy, dst, src):
    copy(
        out=dst.rearrange("p (c i) j -> p c j i", i=4),
        in_=src.rearrange("p j (c i) -> p c j i", i=4),
    )


def tile_picked_cbn_silu_e_kernel(tc, xT, w1, gamma, beta, offs, cls, out):
    nc = tc.nc
    halves = [slice(h * HALF, (h + 1) * HALF) for h in range(2)]
    whole = slice(0, S)

    def vector_gather(dst, src):
        nc.vector.tensor_copy(out=dst, in_=src)

    def scalar_gather(dst, src):
        nc.scalar.activation(out=dst, in_=src, func=COPY)

    with ExitStack() as ctx:
        keep = ctx.enter_context(tc.tile_pool(name="keep", bufs=1))
        psum = ctx.enter_context(tc.psum_pool(name="psum", bufs=1))

        sample_list = keep.tile([P, LIST_COLS], U16, name="sample_list")
        class_list = keep.tile([P, LIST_COLS], U16, name="class_list")

        x_rows = xT.rearrange("(g p j) t -> g p (j t)", g=PASSES, j=PACK)
        x_loads = [(0, 0, 4), (1, 0, 2), (1, 2, 3), (1, 3, 4)]
        x_tiles = [
            keep.tile([P, (j1 - j0) * T], F32, align_bytes=BURST, name="x_%d_%d" % (g, j0)) for g, j0, j1 in x_loads
        ]
        x_plane = {}
        for tile, (g, j0, j1) in zip(x_tiles, x_loads):
            for j in range(j0, j1):
                x_plane[g, j] = tile[:, (j - j0) * T : (j - j0 + 1) * T]
        w_rows = w1.rearrange("(g p j) m -> g p j m", g=PASSES, j=PACK)
        w_raw = [keep.tile([P, PACK, N], F32, align_bytes=BURST, name="w_raw_%d" % g) for g in range(PASSES)]
        gamma_table = [keep.tile([P, U], F32, align_bytes=BURST, name="gamma_%d" % m) for m in range(M_TILES)]
        beta_table = [keep.tile([P, U], F32, align_bytes=BURST, name="beta_%d" % m) for m in range(M_TILES)]

        for n, (g, j0, j1) in enumerate(x_loads):
            nc.sync.dma_start(out=x_tiles[n][:], in_=x_rows[g, :, j0 * T : j1 * T])
            if n == 0:
                nc.sync.dma_start(out=sample_list[:], in_=offs)
        for g in range(PASSES):
            nc.sync.dma_start(out=w_raw[g][:], in_=w_rows[g])
        nc.sync.dma_start(out=class_list[:], in_=cls)
        for m in range(M_TILES):
            nc.sync.dma_start(out=gamma_table[m][:], in_=gamma[m * P : (m + 1) * P, :])
            nc.sync.dma_start(out=beta_table[m][:], in_=beta[m * P : (m + 1) * P, :])

        warm_in = keep.tile([P, 1], F32, name="warm_in")
        warm_out = keep.tile([P, 1], F32, name="warm_out")
        nc.gpsimd.memset(warm_in[:], 0.0)
        nc.scalar.activation(out=warm_out[:], in_=warm_in[:], func=SILU)

        quarters = [(g, m) for g in range(PASSES) for m in range(M_TILES)]
        w_bf = {q: keep.tile([P, P, PACK], BF16, align_bytes=64, name="w_bf_%d_%d" % q) for q in quarters}
        w_scales = {q: keep.tile([P, P], U8, align_bytes=64, name="w_scales_%d_%d" % q) for q in quarters}
        w_codes = {q: keep.tile([P, P], U32, align_bytes=64, name="w_codes_%d_%d" % q) for q in quarters}

        def round_w(copy, g, m, cols=slice(0, P)):
            interleave(copy, w_bf[g, m][:, cols, :], w_raw[g][:, :, m * P + cols.start : m * P + cols.stop])

        def quantize_w(g, m):
            nc.vector.quantize_mx(
                out=w_codes[g, m][:].bitcast(FP8X4),
                scales=w_scales[g, m][:],
                in_=w_bf[g, m][:].rearrange("p m j -> p (m j)"),
            )

        pieces = [(g, h) for g in range(PASSES) for h in range(2)]
        x_scales = {q: keep.tile([P, HALF], U8, align_bytes=64, name="x_scales_%d_%d" % q) for q in pieces}
        picked = {q: keep.tile([P, HALF, PACK], BF16, align_bytes=64, name="picked_%d_%d" % q) for q in pieces}
        dense = [keep.tile([P, PACK - g, S], F32, name="dense_%d" % g) for g in range(PASSES)]
        x_codes = {}

        def sampled(g, j, cols):
            return x_plane[g, j].indirect(sample_list[:, cols.start // 16 : cols.stop // 16])

        def quantize_x(g, h):
            x_codes[g, h] = keep.tile([P, HALF], U32, align_bytes=64, name="x_codes_%d_%d" % (g, h))
            nc.vector.quantize_mx(
                out=x_codes[g, h][:].bitcast(FP8X4),
                scales=x_scales[g, h][:],
                in_=picked[g, h][:].rearrange("p s j -> p (s j)"),
            )

        for j in range(PACK):
            (vector_gather, scalar_gather)[j % 2](dense[0][:, j, :], sampled(0, j, whole))
        interleave(nc.vector.tensor_copy, picked[0, 0][:], dense[0][:, :, halves[0]])
        interleave(nc.scalar.copy, picked[0, 1][:], dense[0][:, :, halves[1]])
        for h in range(2):
            quantize_x(0, h)

        vector_gather(dense[1][:, 0, :], sampled(1, 0, whole))
        scalar_gather(dense[1][:, 1, :], sampled(1, 1, whole))
        vector_gather(dense[1][:, 2, halves[0]], sampled(1, 2, halves[0]))
        scalar_gather(dense[1][:, 2, halves[1]], sampled(1, 2, halves[1]))
        for h, copy in enumerate((nc.vector.tensor_copy, nc.scalar.copy)):
            interleave(copy, picked[1, h][:, :, 0:3], dense[1][:, :, halves[h]])
        vector_gather(picked[1, 0][:, :, 3], sampled(1, 3, halves[0]))
        scalar_gather(picked[1, 1][:, :, 3], sampled(1, 3, halves[1]))
        for h in (1, 0):
            quantize_x(1, h)
        round_w(nc.scalar.copy, 0, 0)
        round_w(nc.scalar.copy, 0, 1)
        quantize_w(0, 0)
        round_w(nc.vector.tensor_copy, 1, 0)
        quantize_w(0, 1)
        quantize_w(1, 0)
        round_w(nc.scalar.copy, 1, 1)
        quantize_w(1, 1)

        y_banks = [
            [psum.tile([P, HALF], F32, name="y_%d_%d" % (m, h)) for h in range(2)] for m in range(M_TILES)
        ]
        for m in range(M_TILES):
            for h in range(2):
                order = list(range(PASSES)) if (m, h) != (1, 1) else list(reversed(range(PASSES)))
                for g in order:
                    nc.tensor.matmul_mx(
                        out=y_banks[m][h][:],
                        lhsT=w_codes[g, m][:].bitcast(FP8X4),
                        lhsT_scale=w_scales[g, m][:],
                        rhs=x_codes[g, h][:].bitcast(FP8X4),
                        rhs_scale=x_scales[g, h][:],
                        start=(g == order[0]),
                        stop=(g == order[-1]),
                    )

        def half_tiles(stem):
            return [keep.tile([P, HALF], F32, align_bytes=BURST, name="%s_%d" % (stem, h)) for h in range(2)]

        def by_class(table, cols):
            return table[:].indirect(class_list[:, cols.start // 16 : cols.stop // 16])

        gamma_0 = half_tiles("gamma_picked_0")
        copied = slice(S - LEAD, S - LEAD + HALF)
        wide_row = keep.tile([P, copied.stop - LEAD + S], F32, align_bytes=BURST, name="wide_row")
        scaled_row = wide_row[:, copied.stop - LEAD :]
        scaled_0 = [scaled_row[:, cols] for cols in halves]
        shifted_row = keep.tile([P, S], F32, name="shifted_0")
        for h, share in enumerate(GAMMA_ON_VECTOR):
            first = h * HALF
            vector_gather(gamma_0[h][:, 0:share], by_class(gamma_table[0], slice(first, first + share)))
            scalar_gather(gamma_0[h][:, share:HALF], by_class(gamma_table[0], slice(first + share, first + HALF)))
        for h in range(2):
            nc.vector.tensor_tensor(out=scaled_0[h], in0=y_banks[0][h][:], in1=gamma_0[h][:], op=MULT)
        shared = slice(S - BETA_ON_SCALAR, S)
        beta_0 = keep.tile([P, BETA_ON_SCALAR], F32, name="beta_picked_0")
        scalar_gather(beta_0[:], by_class(beta_table[0], shared))
        y_1 = wide_row[:, copied]
        for cols in (slice(0, LEAD), slice(LEAD, shared.start)):
            nc.vector.tensor_tensor(
                out=shifted_row[:, cols], in0=by_class(beta_table[0], cols), in1=scaled_row[:, cols], op=ADD
            )
            if cols.start == 0:
                nc.scalar.copy(out=y_1, in_=y_banks[1][0][:])
        nc.vector.tensor_tensor(out=shifted_row[:, shared], in0=beta_0[:], in1=scaled_row[:, shared], op=ADD)

        gamma_1 = keep.tile([P, HALF], F32, name="gamma_picked_1")
        scaled_1 = half_tiles("scaled_1")
        scalar_gather(gamma_1[:], by_class(gamma_table[1], halves[1]))
        for cols in (slice(0, LEAD), slice(LEAD, HALF)):
            nc.vector.tensor_tensor(
                out=scaled_1[0][:, cols], in0=by_class(gamma_table[1], cols), in1=y_1[:, cols], op=MULT
            )
        nc.vector.tensor_tensor(out=scaled_1[1][:], in0=y_banks[1][1][:], in1=gamma_1[:], op=MULT)

        result_0 = wide_row[:, 0:S]
        nc.scalar.activation(out=result_0, in_=shifted_row[:], func=SILU)
        nc.sync.dma_start(out=out[0:P, :], in_=result_0)

        result_1 = half_tiles("result_1")
        shifted_1 = half_tiles("shifted_1")
        beta_1 = keep.tile([P, QUARTER], F32, name="beta_picked_1")
        scalar_gather(beta_1[:], by_class(beta_table[1], slice(S - QUARTER, S)))
        nc.vector.tensor_tensor(
            out=shifted_1[0][:], in0=by_class(beta_table[1], halves[0]), in1=scaled_1[0][:], op=ADD
        )
        nc.scalar.activation(out=result_1[0][:], in_=shifted_1[0][:], func=SILU)
        nc.sync.dma_start(out=out[P:N, halves[0]], in_=result_1[0][:])
        third, fourth = slice(0, QUARTER), slice(QUARTER, HALF)
        nc.vector.tensor_tensor(
            out=shifted_1[1][:, third],
            in0=by_class(beta_table[1], slice(HALF, S - QUARTER)),
            in1=scaled_1[1][:, third],
            op=ADD,
        )
        nc.vector.tensor_tensor(out=shifted_1[1][:, fourth], in0=beta_1[:], in1=scaled_1[1][:, fourth], op=ADD)
        for cols in (third, fourth):
            nc.scalar.activation(out=result_1[1][:, cols], in_=shifted_1[1][:, cols], func=SILU)
        nc.scalar.dma_start(out=out[P:N, halves[1]], in_=result_1[1][:])
